import numpy as np
import ml_dtypes


def mxq(x, axis, fmt="e4m3"):
    dtype, down = {"e4m3": (ml_dtypes.float8_e4m3fn, 7), "e5m2": (ml_dtypes.float8_e5m2, 14)}[fmt]
    v = np.moveaxis(np.asarray(x, np.float32).astype(ml_dtypes.bfloat16).astype(np.float64), axis, -1)
    blocks = v.reshape(v.shape[:-1] + (-1, 32))
    amax = np.abs(blocks).max(-1, keepdims=True)
    byte = np.maximum(np.where(amax > 0, np.frexp(amax)[1] - 1 + 127, 0) - down, 1)
    scale = np.exp2(byte - 127.0)
    codes = (blocks / scale).astype(np.float32).astype(dtype).astype(np.float64)
    return np.moveaxis((codes * scale).reshape(v.shape), -1, axis)


WIDE = False


def mx_kscale(k):
    if not WIDE:
        return np.ones(k)
    levels = np.array([10, -10, 5, -5, 0])
    if k % 512:
        return np.exp2(np.random.permutation(np.resize(levels, k // 32))).repeat(32)
    a = np.empty((k // 512, 16))
    for p in range(k // 512):
        a[p, :8] = np.random.permutation(np.resize(levels, 8))
        for g in range(8):
            far = levels[np.abs(levels - a[p, g]) >= 10]
            a[p, g + 8] = far[np.random.randint(len(far))]
    return np.exp2(a.ravel()).repeat(32)


def f64(x):
    return np.asarray(x).astype(np.float64)


def striped(idx):
    return np.tile(idx.reshape(-1, 16).T, (8, 1)).astype(np.uint16)


def unstriped(offs):
    return offs[:16].T.reshape(-1).astype(np.int64)


E2M1 = np.array([0.0, 0.5, 1.0, 1.5, 2.0, 3.0, 4.0, 6.0, -0.0, -0.5, -1.0, -1.5, -2.0, -3.0, -4.0, -6.0])


def pack_weight(w, fmt):
    k, n = w.shape
    w = f64(np.asarray(w, np.float32).astype(ml_dtypes.bfloat16)).reshape(k // 32, 32, n)
    amax = np.abs(w).max(1)
    if fmt == "e4m3":
        byte = np.frexp(amax)[1] - 1 + 127 - 7
    else:
        mant, ex = np.frexp(amax / 6.0)
        byte = np.where(mant > 0.5, ex, ex - 1) + 127
    byte = np.clip(np.where(amax > 0, byte, 1), 1, 254)
    scaled = (w * np.exp2(127.0 - byte)[:, None, :]).reshape(k, n).astype(np.float32)
    by_word = np.ascontiguousarray(scaled.reshape(k // 512, 128, 4, n).transpose(0, 1, 3, 2))
    if fmt == "e4m3":
        words = by_word.astype(ml_dtypes.float8_e4m3fn).view(np.uint8)
    else:
        c = by_word.astype(ml_dtypes.float4_e2m1fn).view(np.uint8) & 0xF
        words = (c[..., 0::2] | (c[..., 1::2] << 4)).reshape(k // 512, 128, 2 * n)
    return np.ascontiguousarray(words), np.ascontiguousarray(byte.astype(np.uint8).reshape(k // 512, 16, n))


def unpack_weight(words, scales, fmt):
    g, _, n = scales.shape
    words = np.ascontiguousarray(words).reshape(g, 128, n, -1)
    if fmt == "e4m3":
        vals = words.view(ml_dtypes.float8_e4m3fn).astype(np.float64)
    else:
        nib = np.empty((g, 128, n, 4), np.uint8)
        nib[..., 0::2] = words & 0xF
        nib[..., 1::2] = words >> 4
        vals = E2M1[nib]
    vals = vals * np.repeat(np.exp2(scales.astype(np.float64) - 127.0), 8, axis=1)[..., None]
    return vals.transpose(0, 1, 3, 2).reshape(g * 512, n)


K, M, T, S = 512, 128, 4096, 2048


def setup_inputs():
    n = np.random.standard_normal
    s = mx_kscale(K)[:, None]
    u = mx_kscale(512)[:, None]
    v = pack_weight(n((K, T)) * s, "e4m3")
    p_w2 = pack_weight(1.4 * n((512, M)) / np.sqrt(512) / u, "e2m1")
    return {
        "tab_words": v[0],
        "tab_scales": v[1],
        "w1": (n((K, 512)) / np.sqrt(K) / s * u.T).astype(np.float32),
        "w2_words": p_w2[0],
        "w2_scales": p_w2[1],
        "rT": n((M, T)).astype(np.float32),
        "b": (0.3 * n(128)).astype(np.float32),
        "offs": striped(np.random.permutation(T)[:S]),
    }


def reference(tab_words, tab_scales, w1, w2_words, w2_scales, rT, b, offs):
    tab_ = unpack_weight(tab_words, tab_scales, "e4m3")[:, unstriped(offs)]
    w1_ = mxq(f64(w1), 0, "e4m3")
    w2_ = unpack_weight(w2_words, w2_scales, "e2m1")
    h_ = mxq(np.maximum(w1_.T @ tab_, 0.0), 0, "e4m3")
    y = w2_.T @ h_
    return (y + f64(b)[:, None]) + f64(rT)[:, unstriped(offs)]

@@ -1,0 +1,161 @@
+from contextlib import ExitStack
+
+import concourse.mybir as mybir
+
+K, H, M, T, S = 512, 512, 128, 4096, 2048
+FLOPS = 2 * K * H * S + 2 * H * M * S
+
+F32 = mybir.dt.float32
+BF16 = mybir.dt.bfloat16
+I32 = mybir.dt.int32
+U32 = mybir.dt.uint32
+U16 = mybir.dt.uint16
+U8 = mybir.dt.uint8
+FP8X4 = mybir.dt.float8_e4m3fn_x4
+FP4X4 = mybir.dt.float4_e2m1fn_x4
+ADD = mybir.AluOpType.add
+RELU = mybir.ActivationFunctionType.Relu
+
+P = 128
+PACK = 4
+LANES = 16
+CHUNK = 512
+SUB = 128
+HEAD = 512
+
+
+def tile_list_tabres_bias_kernel(
+    tc, tab_words, tab_scales, w1, w2_words, w2_scales, rT, b, offs, out
+):
+    nc = tc.nc
+    with ExitStack() as ctx:
+        keep = ctx.enter_context(tc.tile_pool(name="keep", bufs=1))
+        hpsum = ctx.enter_context(tc.psum_pool(name="hpsum", bufs=5))
+        ypsum = ctx.enter_context(tc.psum_pool(name="ypsum", bufs=3))
+
+        offsets = keep.tile([P, S // LANES], U16, name="offsets")
+        nc.sync.dma_start(offsets[:], offs)
+
+        def picks(lo, hi):
+            return offsets[:, lo // LANES : hi // LANES]
+
+        scale_win = keep.tile([P, T // 4], I32, name="scale_win", align_bytes=64)
+        nc.vector.memset(scale_win[:], 0)
+        tab_scale_rows = tab_scales[0].bitcast(I32)
+        for r in range(4):
+            nc.sync.dma_start(scale_win[r:P:32, :], tab_scale_rows[r:16:4, :])
+
+        w2_plane = keep.tile([P, M // 4], I32, name="w2_plane", align_bytes=64)
+        nc.gpsimd.memset(w2_plane[:], 0)
+        w2_scale_rows = w2_scales[0].bitcast(I32)
+        for r in range(4):
+            nc.gpsimd.dma_start(w2_plane[r:P:32, :], w2_scale_rows[r:16:4, :])
+        bias = keep.tile([P, 1], F32, name="bias", align_bytes=64)
+        nc.gpsimd.dma_start(bias[:], b.rearrange("(p o) -> p o", o=1))
+
+        word_win = keep.tile([P, T], I32, name="word_win", align_bytes=64)
+        tab_word_rows = tab_words[0].rearrange("p t i -> p (t i)").bitcast(I32)
+        nc.sync.dma_start(word_win[:, :HEAD], tab_word_rows[:, :HEAD])
+        w2_codes = keep.tile([P, 2 * M // 4], I32, name="w2_codes", align_bytes=64)
+        nc.sync.dma_start(w2_codes[:], w2_words[0].bitcast(I32))
+        nc.sync.dma_start(word_win[:, HEAD:], tab_word_rows[:, HEAD:])
+        w1_rows = w1.rearrange("(p j) r -> p j r", j=PACK)
+        w1_raw = []
+        for half in range(2):
+            raw = keep.tile([P, PACK, H // 2], F32, name=f"w1_raw{half}", align_bytes=64)
+            nc.sync.dma_start(raw[:], w1_rows[:, :, half * H // 2 : (half + 1) * H // 2])
+            w1_raw.append(raw)
+        res_win = keep.tile([P, T], F32, name="res_win", align_bytes=64)
+        nc.sync.dma_start(res_win[:], rT)
+
+        tok_scales = keep.tile([P, S], U8, name="tok_scales", align_bytes=64)
+        nc.vector.tensor_copy(tok_scales[:], scale_win[:].bitcast(U8).indirect(picks(0, S)))
+
+        w1_bf = keep.tile([P, H * PACK], BF16, name="w1_bf", tag="w1_then_words", align_bytes=64)
+        w1_grouped = w1_bf[:].rearrange("p (t m j) -> p m t j", t=PACK, j=PACK)
+        nc.scalar.copy(w1_grouped[:, : P // 2], w1_raw[0][:].rearrange("p j (m t) -> p m t j", t=PACK))
+        nc.vector.tensor_copy(w1_grouped[:, P // 2 :], w1_raw[1][:].rearrange("p j (m t) -> p m t j", t=PACK))
+        w1_codes = keep.tile([P, H], U32, name="w1_codes", align_bytes=64)
+        w1_plane = keep.tile([P, H], U8, name="w1_plane", align_bytes=64)
+        nc.vector.quantize_mx(out=w1_codes[:].bitcast(FP8X4), scales=w1_plane[:], in_=w1_bf[:])
+
+        words_lo = keep.tile([P, S // 2], U32, name="words_lo", align_bytes=64)
+        words_hi = keep.tile([P, S // 2], U32, name="words_hi", tag="w1_then_words", align_bytes=64)
+        h_bf = keep.tile([P, S * PACK], BF16, name="h_bf", align_bytes=64)
+        h_codes = keep.tile([P, S], U32, name="h_codes", align_bytes=64)
+        h_plane = keep.tile([P, S], U8, name="h_plane", align_bytes=64)
+        res = keep.tile([P, S], F32, name="res", align_bytes=64)
+        total = keep.tile([P, S], F32, name="total", align_bytes=64)
+        y_banks = {}
+
+        def gather_words(lo, hi):
+            tok_words, base = (words_lo, 0) if lo < S // 2 else (words_hi, S // 2)
+            nc.vector.tensor_copy(tok_words[:, lo - base : hi - base], word_win[:].bitcast(U32).indirect(picks(lo, hi)))
+            for s0 in range(lo, hi, SUB):
+                cols = slice(s0, s0 + SUB)
+                bank = hpsum.tile([P, PACK, SUB], F32, name="h_bank")
+                for t in range(PACK):
+                    ch = slice(t * P, (t + 1) * P)
+                    nc.tensor.matmul_mx(
+                        out=bank[:, t, :],
+                        lhsT=w1_codes[:, ch].bitcast(FP8X4),
+                        lhsT_scale=w1_plane[:, ch],
+                        rhs=tok_words[:, s0 - base : s0 - base + SUB].bitcast(FP8X4),
+                        rhs_scale=tok_scales[:, cols],
+                        start=True,
+                        stop=True,
+                    )
+                nc.scalar.activation(
+                    h_bf[:, s0 * PACK : (s0 + SUB) * PACK].rearrange("p (n t) -> p n t", t=PACK),
+                    bank[:].rearrange("p t n -> p n t"),
+                    RELU,
+                )
+
+        def second_product(lo, hi):
+            cols = slice(lo, hi)
+            nc.vector.quantize_mx(
+                out=h_codes[:, cols].bitcast(FP8X4),
+                scales=h_plane[:, cols],
+                in_=h_bf[:, lo * PACK : hi * PACK],
+            )
+            y_bank = ypsum.tile([P, CHUNK], F32, name="y_bank")
+            y_banks[lo] = y_bank
+            nc.tensor.matmul_mx(
+                out=y_bank[:, : hi - lo],
+                lhsT=w2_codes[:].bitcast(U8).bitcast(FP4X4),
+                lhsT_scale=w2_plane[:].bitcast(U8),
+                rhs=h_codes[:, cols].bitcast(FP8X4),
+                rhs_scale=h_plane[:, cols],
+                start=True,
+                stop=True,
+            )
+
+        def gather_residual(lo, hi):
+            nc.vector.tensor_copy(res[:, lo:hi], res_win[:].indirect(picks(lo, hi)))
+
+        def finish(lo, hi):
+            nc.vector.scalar_tensor_tensor(
+                total[:, lo:hi],
+                y_banks[lo][:, : hi - lo],
+                bias[:],
+                res[:, lo:hi],
+                ADD,
+                ADD,
+            )
+            nc.sync.dma_start(out[:, lo:hi], total[:, lo:hi])
+
+        gather_words(0, 512)
+        gather_words(512, 1024)
+        gather_words(1024, 2048)
+        second_product(0, 512)
+        gather_residual(0, 1024)
+        second_product(512, 1024)
+        finish(0, 512)
+        second_product(1024, 1536)
+        finish(512, 1024)
+        gather_residual(1024, 2048)
+        second_product(1536, 1792)
+        finish(1024, 1536)
+        second_product(1792, 2048)
+        finish(1536, 1792)
+        finish(1792, 2048)

@@ -45,14 +45,6 @@ def tile_list_tabres_bias_kernel(
         for r in range(4):
             nc.sync.dma_start(scale_win[r:P:32, :], tab_scale_rows[r:16:4, :])
 
-        w2_plane = keep.tile([P, M // 4], I32, name="w2_plane", align_bytes=64)
-        nc.gpsimd.memset(w2_plane[:], 0)
-        w2_scale_rows = w2_scales[0].bitcast(I32)
-        for r in range(4):
-            nc.gpsimd.dma_start(w2_plane[r:P:32, :], w2_scale_rows[r:16:4, :])
-        bias = keep.tile([P, 1], F32, name="bias", align_bytes=64)
-        nc.gpsimd.dma_start(bias[:], b.rearrange("(p o) -> p o", o=1))
-
         word_win = keep.tile([P, T], I32, name="word_win", align_bytes=64)
         tab_word_rows = tab_words[0].rearrange("p t i -> p (t i)").bitcast(I32)
         nc.sync.dma_start(word_win[:, :HEAD], tab_word_rows[:, :HEAD])
@@ -65,8 +57,16 @@ def tile_list_tabres_bias_kernel(
             raw = keep.tile([P, PACK, H // 2], F32, name=f"w1_raw{half}", align_bytes=64)
             nc.sync.dma_start(raw[:], w1_rows[:, :, half * H // 2 : (half + 1) * H // 2])
             w1_raw.append(raw)
+        w2_plane = keep.tile([P, M // 4], I32, name="w2_plane", align_bytes=64)
+        nc.vector.memset(w2_plane[:], 0)
+        w2_scale_rows = w2_scales[0].bitcast(I32)
+        for r in range(4):
+            nc.sync.dma_start(w2_plane[r:P:32, :], w2_scale_rows[r:16:4, :])
+
         res_win = keep.tile([P, T], F32, name="res_win", align_bytes=64)
         nc.sync.dma_start(res_win[:], rT)
+        bias = keep.tile([P, 1], F32, name="bias", align_bytes=64)
+        nc.sync.dma_start(bias[:], b.rearrange("(p o) -> p o", o=1))
 
         tok_scales = keep.tile([P, S], U8, name="tok_scales", align_bytes=64)
         nc.vector.tensor_copy(tok_scales[:], scale_win[:].bitcast(U8).indirect(picks(0, S)))
@@ -106,8 +106,8 @@ def tile_list_tabres_bias_kernel(
                         stop=True,
                     )
                 nc.scalar.activation(
-                    h_bf[:, s0 * PACK : (s0 + SUB) * PACK].rearrange("p (n t) -> p n t", t=PACK),
-                    bank[:].rearrange("p t n -> p n t"),
+                    h_bf[:, s0 * PACK : (s0 + SUB) * PACK].rearrange("p (c i t) -> p c t i", i=PACK, t=PACK),
+                    bank[:].rearrange("p t (c i) -> p c t i", i=PACK),
                     RELU,
                 )
 

@@ -30,8 +30,8 @@ def tile_list_tabres_bias_kernel(
     nc = tc.nc
     with ExitStack() as ctx:
         keep = ctx.enter_context(tc.tile_pool(name="keep", bufs=1))
-        hpsum = ctx.enter_context(tc.psum_pool(name="hpsum", bufs=5))
-        ypsum = ctx.enter_context(tc.psum_pool(name="ypsum", bufs=3))
+        hpsum = ctx.enter_context(tc.psum_pool(name="hpsum", bufs=6))
+        ypsum = ctx.enter_context(tc.psum_pool(name="ypsum", bufs=2))
 
         offsets = keep.tile([P, S // LANES], U16, name="offsets")
         nc.sync.dma_start(offsets[:], offs)
@@ -50,46 +50,44 @@ def tile_list_tabres_bias_kernel(
         nc.sync.dma_start(word_win[:, :HEAD], tab_word_rows[:, :HEAD])
         w2_codes = keep.tile([P, 2 * M // 4], I32, name="w2_codes", align_bytes=64)
         nc.sync.dma_start(w2_codes[:], w2_words[0].bitcast(I32))
+        w1_raw = keep.tile([P, PACK, H], F32, name="w1_raw", align_bytes=64)
+        nc.sync.dma_start(w1_raw[:], w1.rearrange("(p j) r -> p j r", j=PACK))
         nc.sync.dma_start(word_win[:, HEAD:], tab_word_rows[:, HEAD:])
-        w1_rows = w1.rearrange("(p j) r -> p j r", j=PACK)
-        w1_raw = []
-        for half in range(2):
-            raw = keep.tile([P, PACK, H // 2], F32, name=f"w1_raw{half}", align_bytes=64)
-            nc.sync.dma_start(raw[:], w1_rows[:, :, half * H // 2 : (half + 1) * H // 2])
-            w1_raw.append(raw)
         w2_plane = keep.tile([P, M // 4], I32, name="w2_plane", align_bytes=64)
         nc.vector.memset(w2_plane[:], 0)
         w2_scale_rows = w2_scales[0].bitcast(I32)
         for r in range(4):
             nc.sync.dma_start(w2_plane[r:P:32, :], w2_scale_rows[r:16:4, :])
-
-        res_win = keep.tile([P, T], F32, name="res_win", align_bytes=64)
+        res_win = keep.tile([P, T], F32, name="res_win", tag="residual_then_codes", align_bytes=64)
         nc.sync.dma_start(res_win[:], rT)
+
         bias = keep.tile([P, 1], F32, name="bias", align_bytes=64)
         nc.sync.dma_start(bias[:], b.rearrange("(p o) -> p o", o=1))
 
         tok_scales = keep.tile([P, S], U8, name="tok_scales", align_bytes=64)
         nc.vector.tensor_copy(tok_scales[:], scale_win[:].bitcast(U8).indirect(picks(0, S)))
 
-        w1_bf = keep.tile([P, H * PACK], BF16, name="w1_bf", tag="w1_then_words", align_bytes=64)
-        w1_grouped = w1_bf[:].rearrange("p (t m j) -> p m t j", t=PACK, j=PACK)
-        nc.scalar.copy(w1_grouped[:, : P // 2], w1_raw[0][:].rearrange("p j (m t) -> p m t j", t=PACK))
-        nc.vector.tensor_copy(w1_grouped[:, P // 2 :], w1_raw[1][:].rearrange("p j (m t) -> p m t j", t=PACK))
+        w1_bf = keep.tile([P, H * PACK], BF16, name="w1_bf", align_bytes=64)
+        nc.scalar.copy(
+            w1_bf[:].rearrange("p (t m j) -> p m t j", t=PACK, j=PACK),
+            w1_raw[:].rearrange("p j (m t) -> p m t j", t=PACK),
+        )
         w1_codes = keep.tile([P, H], U32, name="w1_codes", align_bytes=64)
         w1_plane = keep.tile([P, H], U8, name="w1_plane", align_bytes=64)
         nc.vector.quantize_mx(out=w1_codes[:].bitcast(FP8X4), scales=w1_plane[:], in_=w1_bf[:])
 
-        words_lo = keep.tile([P, S // 2], U32, name="words_lo", align_bytes=64)
-        words_hi = keep.tile([P, S // 2], U32, name="words_hi", tag="w1_then_words", align_bytes=64)
+        words_lo = keep.tile([P, S - CHUNK], U32, name="words_lo", align_bytes=64)
+        words_hi = keep.tile([P, CHUNK], U32, name="words_hi", align_bytes=64)
         h_bf = keep.tile([P, S * PACK], BF16, name="h_bf", align_bytes=64)
-        h_codes = keep.tile([P, S], U32, name="h_codes", align_bytes=64)
+        h_first = keep.tile([P, CHUNK], U32, name="h_first", align_bytes=64)
+        h_rest = keep.tile([P, S - CHUNK], U32, name="h_rest", tag="residual_then_codes", align_bytes=64)
         h_plane = keep.tile([P, S], U8, name="h_plane", align_bytes=64)
         res = keep.tile([P, S], F32, name="res", align_bytes=64)
         total = keep.tile([P, S], F32, name="total", align_bytes=64)
         y_banks = {}
 
         def gather_words(lo, hi):
-            tok_words, base = (words_lo, 0) if lo < S // 2 else (words_hi, S // 2)
+            tok_words, base = (words_lo, 0) if lo < S - CHUNK else (words_hi, S - CHUNK)
             nc.vector.tensor_copy(tok_words[:, lo - base : hi - base], word_win[:].bitcast(U32).indirect(picks(lo, hi)))
             for s0 in range(lo, hi, SUB):
                 cols = slice(s0, s0 + SUB)
@@ -113,8 +111,9 @@ def tile_list_tabres_bias_kernel(
 
         def second_product(lo, hi):
             cols = slice(lo, hi)
+            h_codes = h_first[:, cols] if lo < CHUNK else h_rest[:, lo - CHUNK : hi - CHUNK]
             nc.vector.quantize_mx(
-                out=h_codes[:, cols].bitcast(FP8X4),
+                out=h_codes.bitcast(FP8X4),
                 scales=h_plane[:, cols],
                 in_=h_bf[:, lo * PACK : hi * PACK],
             )
@@ -124,7 +123,7 @@ def tile_list_tabres_bias_kernel(
                 out=y_bank[:, : hi - lo],
                 lhsT=w2_codes[:].bitcast(U8).bitcast(FP4X4),
                 lhsT_scale=w2_plane[:].bitcast(U8),
-                rhs=h_codes[:, cols].bitcast(FP8X4),
+                rhs=h_codes.bitcast(FP8X4),
                 rhs_scale=h_plane[:, cols],
                 start=True,
                 stop=True,
@@ -146,14 +145,14 @@ def tile_list_tabres_bias_kernel(
 
         gather_words(0, 512)
         gather_words(512, 1024)
-        gather_words(1024, 2048)
+        gather_words(1024, 1536)
+        gather_words(1536, 2048)
         second_product(0, 512)
-        gather_residual(0, 1024)
+        gather_residual(0, 2048)
         second_product(512, 1024)
         finish(0, 512)
         second_product(1024, 1536)
         finish(512, 1024)
-        gather_residual(1024, 2048)
         second_product(1536, 1792)
         finish(1024, 1536)
         second_product(1792, 2048)

@@ -14,6 +14,7 @@ U8 = mybir.dt.uint8
 FP8X4 = mybir.dt.float8_e4m3fn_x4
 FP4X4 = mybir.dt.float4_e2m1fn_x4
 ADD = mybir.AluOpType.add
+IDENTITY = mybir.ActivationFunctionType.Identity
 RELU = mybir.ActivationFunctionType.Relu
 
 P = 128
@@ -48,8 +49,8 @@ def tile_list_tabres_bias_kernel(
         word_win = keep.tile([P, T], I32, name="word_win", align_bytes=64)
         tab_word_rows = tab_words[0].rearrange("p t i -> p (t i)").bitcast(I32)
         nc.sync.dma_start(word_win[:, :HEAD], tab_word_rows[:, :HEAD])
-        w2_codes = keep.tile([P, 2 * M // 4], I32, name="w2_codes", align_bytes=64)
-        nc.sync.dma_start(w2_codes[:], w2_words[0].bitcast(I32))
+        bias = keep.tile([P, 1], F32, name="bias", align_bytes=64)
+        nc.sync.dma_start(bias[:], b.rearrange("(p o) -> p o", o=1))
         w1_raw = keep.tile([P, PACK, H], F32, name="w1_raw", align_bytes=64)
         nc.sync.dma_start(w1_raw[:], w1.rearrange("(p j) r -> p j r", j=PACK))
         nc.sync.dma_start(word_win[:, HEAD:], tab_word_rows[:, HEAD:])
@@ -58,11 +59,11 @@ def tile_list_tabres_bias_kernel(
         w2_scale_rows = w2_scales[0].bitcast(I32)
         for r in range(4):
             nc.sync.dma_start(w2_plane[r:P:32, :], w2_scale_rows[r:16:4, :])
+        w2_codes = keep.tile([P, 2 * M // 4], I32, name="w2_codes", align_bytes=64)
+        nc.sync.dma_start(w2_codes[:], w2_words[0].bitcast(I32))
         res_win = keep.tile([P, T], F32, name="res_win", tag="residual_then_codes", align_bytes=64)
         nc.sync.dma_start(res_win[:], rT)
 
-        bias = keep.tile([P, 1], F32, name="bias", align_bytes=64)
-        nc.sync.dma_start(bias[:], b.rearrange("(p o) -> p o", o=1))
 
         tok_scales = keep.tile([P, S], U8, name="tok_scales", align_bytes=64)
         nc.vector.tensor_copy(tok_scales[:], scale_win[:].bitcast(U8).indirect(picks(0, S)))
@@ -84,11 +85,15 @@ def tile_list_tabres_bias_kernel(
         h_plane = keep.tile([P, S], U8, name="h_plane", align_bytes=64)
         res = keep.tile([P, S], F32, name="res", align_bytes=64)
         total = keep.tile([P, S], F32, name="total", align_bytes=64)
+        y_biased = keep.tile([P, CHUNK], F32, name="y_biased", align_bytes=64)
         y_banks = {}
 
         def gather_words(lo, hi):
             tok_words, base = (words_lo, 0) if lo < S - CHUNK else (words_hi, S - CHUNK)
             nc.vector.tensor_copy(tok_words[:, lo - base : hi - base], word_win[:].bitcast(U32).indirect(picks(lo, hi)))
+
+        def first_product(lo, hi):
+            tok_words, base = (words_lo, 0) if lo < S - CHUNK else (words_hi, S - CHUNK)
             for s0 in range(lo, hi, SUB):
                 cols = slice(s0, s0 + SUB)
                 bank = hpsum.tile([P, PACK, SUB], F32, name="h_bank")
@@ -132,6 +137,10 @@ def tile_list_tabres_bias_kernel(
         def gather_residual(lo, hi):
             nc.vector.tensor_copy(res[:, lo:hi], res_win[:].indirect(picks(lo, hi)))
 
+        def finish_aside(lo, hi):
+            nc.gpsimd.tensor_tensor(total[:, lo:hi], y_biased[:], res[:, lo:hi], ADD)
+            nc.sync.dma_start(out[:, lo:hi], total[:, lo:hi])
+
         def finish(lo, hi):
             nc.vector.scalar_tensor_tensor(
                 total[:, lo:hi],
@@ -143,14 +152,17 @@ def tile_list_tabres_bias_kernel(
             )
             nc.sync.dma_start(out[:, lo:hi], total[:, lo:hi])
 
-        gather_words(0, 512)
-        gather_words(512, 1024)
-        gather_words(1024, 1536)
-        gather_words(1536, 2048)
+        for lo in range(0, S, CHUNK):
+            gather_words(lo, lo + CHUNK)
+        first_product(0, 512)
         second_product(0, 512)
-        gather_residual(0, 2048)
+        nc.scalar.activation(y_biased[:], y_banks[0][:], IDENTITY, bias=bias[:])
+        first_product(512, 1536)
+        first_product(1536, 2048)
+        gather_residual(0, 512)
+        finish_aside(0, 512)
+        gather_residual(512, 2048)
         second_product(512, 1024)
-        finish(0, 512)
         second_product(1024, 1536)
         finish(512, 1024)
         second_product(1536, 1792)

@@ -23,6 +23,7 @@ LANES = 16
 CHUNK = 512
 SUB = 128
 HEAD = 512
+RES_HEAD = 1024
 
 
 def tile_list_tabres_bias_kernel(
@@ -31,8 +32,8 @@ def tile_list_tabres_bias_kernel(
     nc = tc.nc
     with ExitStack() as ctx:
         keep = ctx.enter_context(tc.tile_pool(name="keep", bufs=1))
-        hpsum = ctx.enter_context(tc.psum_pool(name="hpsum", bufs=6))
-        ypsum = ctx.enter_context(tc.psum_pool(name="ypsum", bufs=2))
+        hpsum = ctx.enter_context(tc.psum_pool(name="hpsum", bufs=3))
+        ypsum = ctx.enter_context(tc.psum_pool(name="ypsum", bufs=3))
 
         offsets = keep.tile([P, S // LANES], U16, name="offsets")
         nc.sync.dma_start(offsets[:], offs)
@@ -42,31 +43,35 @@ def tile_list_tabres_bias_kernel(
 
         scale_win = keep.tile([P, T // 4], I32, name="scale_win", align_bytes=64)
         nc.vector.memset(scale_win[:], 0)
-        tab_scale_rows = tab_scales[0].bitcast(I32)
-        for r in range(4):
-            nc.sync.dma_start(scale_win[r:P:32, :], tab_scale_rows[r:16:4, :])
+        nc.sync.dma_start(scale_win[0:P:8, :], tab_scales[0].bitcast(I32))
+        w2_plane = keep.tile([P, M // 4], I32, name="w2_plane", align_bytes=64)
+        nc.vector.memset(w2_plane[:], 0)
+        tok_plane = keep.tile([P, S // 4], I32, name="tok_plane", align_bytes=64)
+        nc.vector.memset(tok_plane[:], 0)
 
         word_win = keep.tile([P, T], I32, name="word_win", align_bytes=64)
         tab_word_rows = tab_words[0].rearrange("p t i -> p (t i)").bitcast(I32)
         nc.sync.dma_start(word_win[:, :HEAD], tab_word_rows[:, :HEAD])
-        bias = keep.tile([P, 1], F32, name="bias", align_bytes=64)
-        nc.sync.dma_start(bias[:], b.rearrange("(p o) -> p o", o=1))
+        w2_codes = keep.tile([P, 2 * M // 4], I32, name="w2_codes", align_bytes=64)
+        nc.sync.dma_start(w2_codes[:], w2_words[0].bitcast(I32))
         w1_raw = keep.tile([P, PACK, H], F32, name="w1_raw", align_bytes=64)
         nc.sync.dma_start(w1_raw[:], w1.rearrange("(p j) r -> p j r", j=PACK))
-        nc.sync.dma_start(word_win[:, HEAD:], tab_word_rows[:, HEAD:])
-        w2_plane = keep.tile([P, M // 4], I32, name="w2_plane", align_bytes=64)
-        nc.vector.memset(w2_plane[:], 0)
         w2_scale_rows = w2_scales[0].bitcast(I32)
         for r in range(4):
             nc.sync.dma_start(w2_plane[r:P:32, :], w2_scale_rows[r:16:4, :])
-        w2_codes = keep.tile([P, 2 * M // 4], I32, name="w2_codes", align_bytes=64)
-        nc.sync.dma_start(w2_codes[:], w2_words[0].bitcast(I32))
+        nc.sync.dma_start(word_win[:, HEAD:], tab_word_rows[:, HEAD:])
+        bias = keep.tile([P, 1], F32, name="bias", align_bytes=64)
+        nc.sync.dma_start(bias[:], b.rearrange("(p o) -> p o", o=1))
+
         res_win = keep.tile([P, T], F32, name="res_win", tag="residual_then_codes", align_bytes=64)
-        nc.sync.dma_start(res_win[:], rT)
+        nc.sync.dma_start(res_win[:, :RES_HEAD], rT[:, :RES_HEAD])
 
-
-        tok_scales = keep.tile([P, S], U8, name="tok_scales", align_bytes=64)
-        nc.vector.tensor_copy(tok_scales[:], scale_win[:].bitcast(U8).indirect(picks(0, S)))
+        picked_scales = keep.tile([P, S], U8, name="picked_scales", align_bytes=64)
+        nc.vector.tensor_copy(picked_scales[:], scale_win[:].bitcast(U8).indirect(picks(0, S)))
+        for r in range(4):
+            nc.sync.dma_start(tok_plane[r:P:32, :], picked_scales[:].bitcast(I32)[8 * r : P : 32, :])
+        tok_scales = tok_plane[:].bitcast(U8)
+        nc.sync.dma_start(res_win[:, RES_HEAD:], rT[:, RES_HEAD:])
 
         w1_bf = keep.tile([P, H * PACK], BF16, name="w1_bf", align_bytes=64)
         nc.scalar.copy(
@@ -77,25 +82,21 @@ def tile_list_tabres_bias_kernel(
         w1_plane = keep.tile([P, H], U8, name="w1_plane", align_bytes=64)
         nc.vector.quantize_mx(out=w1_codes[:].bitcast(FP8X4), scales=w1_plane[:], in_=w1_bf[:])
 
-        words_lo = keep.tile([P, S - CHUNK], U32, name="words_lo", align_bytes=64)
-        words_hi = keep.tile([P, CHUNK], U32, name="words_hi", align_bytes=64)
-        h_bf = keep.tile([P, S * PACK], BF16, name="h_bf", align_bytes=64)
-        h_first = keep.tile([P, CHUNK], U32, name="h_first", align_bytes=64)
-        h_rest = keep.tile([P, S - CHUNK], U32, name="h_rest", tag="residual_then_codes", align_bytes=64)
-        h_plane = keep.tile([P, S], U8, name="h_plane", align_bytes=64)
-        res = keep.tile([P, S], F32, name="res", align_bytes=64)
+        tok_words = [
+            keep.tile([P, CHUNK], U32, name=f"tok_words{c}", tag=f"words{c}", align_bytes=64) for c in range(S // CHUNK)
+        ]
+        h_bf = [
+            keep.tile([P, CHUNK * PACK], BF16, name=f"h_bf{c}", tag=f"h{c}", align_bytes=64) for c in range(S // CHUNK)
+        ]
         total = keep.tile([P, S], F32, name="total", align_bytes=64)
-        y_biased = keep.tile([P, CHUNK], F32, name="y_biased", align_bytes=64)
         y_banks = {}
 
-        def gather_words(lo, hi):
-            tok_words, base = (words_lo, 0) if lo < S - CHUNK else (words_hi, S - CHUNK)
-            nc.vector.tensor_copy(tok_words[:, lo - base : hi - base], word_win[:].bitcast(U32).indirect(picks(lo, hi)))
+        def gather_words(c):
+            nc.vector.tensor_copy(tok_words[c][:], word_win[:].bitcast(U32).indirect(picks(c * CHUNK, (c + 1) * CHUNK)))
 
-        def first_product(lo, hi):
-            tok_words, base = (words_lo, 0) if lo < S - CHUNK else (words_hi, S - CHUNK)
-            for s0 in range(lo, hi, SUB):
-                cols = slice(s0, s0 + SUB)
+        def first_product(c):
+            for s0 in range(0, CHUNK, SUB):
+                cols = slice(c * CHUNK + s0, c * CHUNK + s0 + SUB)
                 bank = hpsum.tile([P, PACK, SUB], F32, name="h_bank")
                 for t in range(PACK):
                     ch = slice(t * P, (t + 1) * P)
@@ -103,24 +104,23 @@ def tile_list_tabres_bias_kernel(
                         out=bank[:, t, :],
                         lhsT=w1_codes[:, ch].bitcast(FP8X4),
                         lhsT_scale=w1_plane[:, ch],
-                        rhs=tok_words[:, s0 - base : s0 - base + SUB].bitcast(FP8X4),
+                        rhs=tok_words[c][:, s0 : s0 + SUB].bitcast(FP8X4),
                         rhs_scale=tok_scales[:, cols],
                         start=True,
                         stop=True,
                     )
                 nc.scalar.activation(
-                    h_bf[:, s0 * PACK : (s0 + SUB) * PACK].rearrange("p (c i t) -> p c t i", i=PACK, t=PACK),
-                    bank[:].rearrange("p t (c i) -> p c t i", i=PACK),
+                    h_bf[c][:, s0 * PACK : (s0 + SUB) * PACK].rearrange("p (n t) -> p n t", t=PACK),
+                    bank[:].rearrange("p t n -> p n t"),
                     RELU,
                 )
 
-        def second_product(lo, hi):
-            cols = slice(lo, hi)
-            h_codes = h_first[:, cols] if lo < CHUNK else h_rest[:, lo - CHUNK : hi - CHUNK]
+        def second_product(lo, hi, h_codes, h_plane):
+            base = lo % CHUNK
             nc.vector.quantize_mx(
                 out=h_codes.bitcast(FP8X4),
-                scales=h_plane[:, cols],
-                in_=h_bf[:, lo * PACK : hi * PACK],
+                scales=h_plane,
+                in_=h_bf[lo // CHUNK][:, base * PACK : (base + hi - lo) * PACK],
             )
             y_bank = ypsum.tile([P, CHUNK], F32, name="y_bank")
             y_banks[lo] = y_bank
@@ -129,44 +129,44 @@ def tile_list_tabres_bias_kernel(
                 lhsT=w2_codes[:].bitcast(U8).bitcast(FP4X4),
                 lhsT_scale=w2_plane[:].bitcast(U8),
                 rhs=h_codes.bitcast(FP8X4),
-                rhs_scale=h_plane[:, cols],
+                rhs_scale=h_plane,
                 start=True,
                 stop=True,
             )
 
-        def gather_residual(lo, hi):
-            nc.vector.tensor_copy(res[:, lo:hi], res_win[:].indirect(picks(lo, hi)))
+        def gather_residual(dst, lo, hi):
+            nc.vector.tensor_copy(dst, res_win[:].indirect(picks(lo, hi)))
 
-        def finish_aside(lo, hi):
-            nc.gpsimd.tensor_tensor(total[:, lo:hi], y_biased[:], res[:, lo:hi], ADD)
+        def finish_aside(lo, hi, y_biased, res):
+            nc.scalar.activation(y_biased, y_banks[lo][:], IDENTITY, bias=bias[:])
+            nc.gpsimd.tensor_tensor(total[:, lo:hi], y_biased, res, ADD)
             nc.sync.dma_start(out[:, lo:hi], total[:, lo:hi])
 
-        def finish(lo, hi):
-            nc.vector.scalar_tensor_tensor(
-                total[:, lo:hi],
-                y_banks[lo][:, : hi - lo],
-                bias[:],
-                res[:, lo:hi],
-                ADD,
-                ADD,
-            )
+        def finish(lo, hi, res):
+            base = max(k for k in y_banks if k <= lo)
+            nc.vector.scalar_tensor_tensor(total[:, lo:hi], y_banks[base][:, lo - base : hi - base], bias[:], res, ADD, ADD)
             nc.sync.dma_start(out[:, lo:hi], total[:, lo:hi])
 
-        for lo in range(0, S, CHUNK):
-            gather_words(lo, lo + CHUNK)
-        first_product(0, 512)
-        second_product(0, 512)
-        nc.scalar.activation(y_biased[:], y_banks[0][:], IDENTITY, bias=bias[:])
-        first_product(512, 1536)
-        first_product(1536, 2048)
-        gather_residual(0, 512)
-        finish_aside(0, 512)
-        gather_residual(512, 2048)
-        second_product(512, 1024)
-        second_product(1024, 1536)
-        finish(512, 1024)
-        second_product(1536, 1792)
-        finish(1024, 1536)
-        second_product(1792, 2048)
-        finish(1536, 1792)
-        finish(1792, 2048)
+        for c in range(S // CHUNK):
+            gather_words(c)
+        h_first = keep.tile([P, CHUNK], U32, name="h_first", align_bytes=64)
+        res = keep.tile([P, S], F32, name="res", align_bytes=64)
+        first_product(0)
+        plane_first = keep.tile([P, CHUNK], U8, name="plane_first", align_bytes=64)
+        second_product(0, 512, h_first[:], plane_first[:])
+        first_product(1)
+        gather_residual(res[:, :512], 0, 512)
+        y_first = keep.tile([P, CHUNK], F32, name="y_first", align_bytes=64)
+        finish_aside(0, 512, y_first[:], res[:, :512])
+        first_product(2)
+        first_product(3)
+        gather_residual(res[:, 512:], 512, 2048)
+        h_rest = keep.tile([P, S - CHUNK], U32, name="h_rest", tag="residual_then_codes", align_bytes=64)
+        plane_rest = keep.tile([P, S - CHUNK], U8, name="plane_rest", tag="words3", align_bytes=64)
+        second_product(512, 1024, h_rest[:, :512], plane_rest[:, :512])
+        second_product(1024, 1536, h_rest[:, 512:1024], plane_rest[:, 512:1024])
+        second_product(1536, 2048, h_rest[:, 1024:], plane_rest[:, 1024:])
+        finish(512, 1024, res[:, 512:1024])
+        finish(1024, 1536, res[:, 1024:1536])
+        finish(1536, 1792, res[:, 1536:1792])
+        finish(1792, 2048, res[:, 1792:])

@@ -24,6 +24,7 @@ CHUNK = 512
 SUB = 128
 HEAD = 512
 RES_HEAD = 1024
+H_BANKS = 4
 
 
 def tile_list_tabres_bias_kernel(
@@ -32,8 +33,7 @@ def tile_list_tabres_bias_kernel(
     nc = tc.nc
     with ExitStack() as ctx:
         keep = ctx.enter_context(tc.tile_pool(name="keep", bufs=1))
-        hpsum = ctx.enter_context(tc.psum_pool(name="hpsum", bufs=3))
-        ypsum = ctx.enter_context(tc.psum_pool(name="ypsum", bufs=3))
+        psum = ctx.enter_context(tc.psum_pool(name="psum", bufs=1))
 
         offsets = keep.tile([P, S // LANES], U16, name="offsets")
         nc.sync.dma_start(offsets[:], offs)
@@ -63,7 +63,7 @@ def tile_list_tabres_bias_kernel(
         bias = keep.tile([P, 1], F32, name="bias", align_bytes=64)
         nc.sync.dma_start(bias[:], b.rearrange("(p o) -> p o", o=1))
 
-        res_win = keep.tile([P, T], F32, name="res_win", tag="residual_then_codes", align_bytes=64)
+        res_win = keep.tile([P, T], F32, name="res_win", align_bytes=64)
         nc.sync.dma_start(res_win[:, :RES_HEAD], rT[:, :RES_HEAD])
 
         picked_scales = keep.tile([P, S], U8, name="picked_scales", align_bytes=64)
@@ -97,7 +97,7 @@ def tile_list_tabres_bias_kernel(
         def first_product(c):
             for s0 in range(0, CHUNK, SUB):
                 cols = slice(c * CHUNK + s0, c * CHUNK + s0 + SUB)
-                bank = hpsum.tile([P, PACK, SUB], F32, name="h_bank")
+                bank = psum.tile([P, PACK, SUB], F32, name="h_bank", tag=f"bank{cols.start // SUB % H_BANKS}")
                 for t in range(PACK):
                     ch = slice(t * P, (t + 1) * P)
                     nc.tensor.matmul_mx(
@@ -115,14 +115,14 @@ def tile_list_tabres_bias_kernel(
                     RELU,
                 )
 
-        def second_product(lo, hi, h_codes, h_plane):
+        def second_product(lo, hi, h_codes, h_plane, bank_no):
             base = lo % CHUNK
             nc.vector.quantize_mx(
                 out=h_codes.bitcast(FP8X4),
                 scales=h_plane,
                 in_=h_bf[lo // CHUNK][:, base * PACK : (base + hi - lo) * PACK],
             )
-            y_bank = ypsum.tile([P, CHUNK], F32, name="y_bank")
+            y_bank = psum.tile([P, CHUNK], F32, name="y_bank", tag=f"bank{bank_no}")
             y_banks[lo] = y_bank
             nc.tensor.matmul_mx(
                 out=y_bank[:, : hi - lo],
@@ -153,7 +153,7 @@ def tile_list_tabres_bias_kernel(
         res = keep.tile([P, S], F32, name="res", align_bytes=64)
         first_product(0)
         plane_first = keep.tile([P, CHUNK], U8, name="plane_first", align_bytes=64)
-        second_product(0, 512, h_first[:], plane_first[:])
+        second_product(0, 512, h_first[:], plane_first[:], 4)
         first_product(1)
         gather_residual(res[:, :512], 0, 512)
         y_first = keep.tile([P, CHUNK], F32, name="y_first", align_bytes=64)
@@ -161,12 +161,14 @@ def tile_list_tabres_bias_kernel(
         first_product(2)
         first_product(3)
         gather_residual(res[:, 512:], 512, 2048)
-        h_rest = keep.tile([P, S - CHUNK], U32, name="h_rest", tag="residual_then_codes", align_bytes=64)
+        h_rest = keep.tile([P, S - CHUNK], U32, name="h_rest", align_bytes=64)
         plane_rest = keep.tile([P, S - CHUNK], U8, name="plane_rest", tag="words3", align_bytes=64)
-        second_product(512, 1024, h_rest[:, :512], plane_rest[:, :512])
-        second_product(1024, 1536, h_rest[:, 512:1024], plane_rest[:, 512:1024])
-        second_product(1536, 2048, h_rest[:, 1024:], plane_rest[:, 1024:])
+        second_product(512, 1024, h_rest[:, :512], plane_rest[:, :512], 5)
+        second_product(1024, 1536, h_rest[:, 512:1024], plane_rest[:, 512:1024], H_BANKS - 1)
+        second_product(1536, 1792, h_rest[:, 1024:1280], plane_rest[:, 1024:1280], 6)
+        second_product(1792, 2048, h_rest[:, 1280:], plane_rest[:, 1280:], 7)
         finish(512, 1024, res[:, 512:1024])
-        finish(1024, 1536, res[:, 1024:1536])
+        finish(1024, 1280, res[:, 1024:1280])
+        finish(1280, 1536, res[:, 1280:1536])
         finish(1536, 1792, res[:, 1536:1792])
         finish(1792, 2048, res[:, 1792:])

@@ -23,7 +23,7 @@ LANES = 16
 CHUNK = 512
 SUB = 128
 HEAD = 512
-RES_HEAD = 1024
+RES_HEAD = 512
 H_BANKS = 4
 
 

@@ -22,7 +22,7 @@ PACK = 4
 LANES = 16
 CHUNK = 512
 SUB = 128
-HEAD = 512
+SCALE_ROW0 = 112
 RES_HEAD = 512
 H_BANKS = 4
 
@@ -35,33 +35,29 @@ def tile_list_tabres_bias_kernel(
         keep = ctx.enter_context(tc.tile_pool(name="keep", bufs=1))
         psum = ctx.enter_context(tc.psum_pool(name="psum", bufs=1))
 
+        scale_win = keep.tile([P, T // 4], I32, name="scale_win", align_bytes=64)
+        nc.sync.dma_start(scale_win[SCALE_ROW0:P, :], tab_scales[0].bitcast(I32))
         offsets = keep.tile([P, S // LANES], U16, name="offsets")
         nc.sync.dma_start(offsets[:], offs)
 
         def picks(lo, hi):
             return offsets[:, lo // LANES : hi // LANES]
 
-        scale_win = keep.tile([P, T // 4], I32, name="scale_win", align_bytes=64)
-        nc.vector.memset(scale_win[:], 0)
-        nc.sync.dma_start(scale_win[0:P:8, :], tab_scales[0].bitcast(I32))
         w2_plane = keep.tile([P, M // 4], I32, name="w2_plane", align_bytes=64)
         nc.vector.memset(w2_plane[:], 0)
+        nc.vector.memset(scale_win[0:SCALE_ROW0, :], 0)
         tok_plane = keep.tile([P, S // 4], I32, name="tok_plane", align_bytes=64)
         nc.vector.memset(tok_plane[:], 0)
 
-        word_win = keep.tile([P, T], I32, name="word_win", align_bytes=64)
-        tab_word_rows = tab_words[0].rearrange("p t i -> p (t i)").bitcast(I32)
-        nc.sync.dma_start(word_win[:, :HEAD], tab_word_rows[:, :HEAD])
-        w2_codes = keep.tile([P, 2 * M // 4], I32, name="w2_codes", align_bytes=64)
-        nc.sync.dma_start(w2_codes[:], w2_words[0].bitcast(I32))
         w1_raw = keep.tile([P, PACK, H], F32, name="w1_raw", align_bytes=64)
         nc.sync.dma_start(w1_raw[:], w1.rearrange("(p j) r -> p j r", j=PACK))
         w2_scale_rows = w2_scales[0].bitcast(I32)
         for r in range(4):
             nc.sync.dma_start(w2_plane[r:P:32, :], w2_scale_rows[r:16:4, :])
-        nc.sync.dma_start(word_win[:, HEAD:], tab_word_rows[:, HEAD:])
-        bias = keep.tile([P, 1], F32, name="bias", align_bytes=64)
-        nc.sync.dma_start(bias[:], b.rearrange("(p o) -> p o", o=1))
+        word_win = keep.tile([P, T], I32, name="word_win", align_bytes=64)
+        nc.sync.dma_start(word_win[:], tab_words[0].rearrange("p t i -> p (t i)").bitcast(I32))
+        w2_codes = keep.tile([P, 2 * M // 4], I32, name="w2_codes", align_bytes=64)
+        nc.sync.dma_start(w2_codes[:], w2_words[0].bitcast(I32))
 
         res_win = keep.tile([P, T], F32, name="res_win", align_bytes=64)
         nc.sync.dma_start(res_win[:, :RES_HEAD], rT[:, :RES_HEAD])
@@ -69,9 +65,11 @@ def tile_list_tabres_bias_kernel(
         picked_scales = keep.tile([P, S], U8, name="picked_scales", align_bytes=64)
         nc.vector.tensor_copy(picked_scales[:], scale_win[:].bitcast(U8).indirect(picks(0, S)))
         for r in range(4):
-            nc.sync.dma_start(tok_plane[r:P:32, :], picked_scales[:].bitcast(I32)[8 * r : P : 32, :])
+            nc.sync.dma_start(tok_plane[r:P:32, :], picked_scales[:].bitcast(I32)[SCALE_ROW0 + r : P : 4, :])
         tok_scales = tok_plane[:].bitcast(U8)
         nc.sync.dma_start(res_win[:, RES_HEAD:], rT[:, RES_HEAD:])
+        bias = keep.tile([P, 1], F32, name="bias", align_bytes=64)
+        nc.sync.dma_start(bias[:], b.rearrange("(p o) -> p o", o=1))
 
         w1_bf = keep.tile([P, H * PACK], BF16, name="w1_bf", align_bytes=64)
         nc.scalar.copy(

@@ -113,21 +113,28 @@ def tile_list_tabres_bias_kernel(
                     RELU,
                 )
 
-        def second_product(lo, hi, h_codes, h_plane, bank_no):
+        h_codes = keep.tile([P, S], U32, name="h_codes", align_bytes=64)
+        h_plane = keep.tile([P, S], U8, name="h_plane", align_bytes=64)
+
+        def quantise_h(lo, hi):
             base = lo % CHUNK
             nc.vector.quantize_mx(
-                out=h_codes.bitcast(FP8X4),
-                scales=h_plane,
+                out=h_codes[:, lo:hi].bitcast(FP8X4),
+                scales=h_plane[:, lo:hi],
                 in_=h_bf[lo // CHUNK][:, base * PACK : (base + hi - lo) * PACK],
             )
-            y_bank = psum.tile([P, CHUNK], F32, name="y_bank", tag=f"bank{bank_no}")
-            y_banks[lo] = y_bank
+
+        def open_bank(lo, bank_no):
+            y_banks[lo] = psum.tile([P, CHUNK], F32, name=f"y_bank{lo}", tag=f"bank{bank_no}")
+
+        def second_product(lo, hi):
+            base = max(k for k in y_banks if k <= lo)
             nc.tensor.matmul_mx(
-                out=y_bank[:, : hi - lo],
+                out=y_banks[base][:, lo - base : hi - base],
                 lhsT=w2_codes[:].bitcast(U8).bitcast(FP4X4),
                 lhsT_scale=w2_plane[:].bitcast(U8),
-                rhs=h_codes.bitcast(FP8X4),
-                rhs_scale=h_plane,
+                rhs=h_codes[:, lo:hi].bitcast(FP8X4),
+                rhs_scale=h_plane[:, lo:hi],
                 start=True,
                 stop=True,
             )
@@ -135,9 +142,11 @@ def tile_list_tabres_bias_kernel(
         def gather_residual(dst, lo, hi):
             nc.vector.tensor_copy(dst, res_win[:].indirect(picks(lo, hi)))
 
-        def finish_aside(lo, hi, y_biased, res):
-            nc.scalar.activation(y_biased, y_banks[lo][:], IDENTITY, bias=bias[:])
-            nc.gpsimd.tensor_tensor(total[:, lo:hi], y_biased, res, ADD)
+        def bring_out(lo, hi, y_biased):
+            nc.scalar.activation(y_biased, y_banks[lo][:, : hi - lo], IDENTITY, bias=bias[:])
+
+        def finish_fused(lo, hi, y_biased):
+            nc.vector.tensor_tensor(total[:, lo:hi], res_win[:].indirect(picks(lo, hi)), y_biased, ADD)
             nc.sync.dma_start(out[:, lo:hi], total[:, lo:hi])
 
         def finish(lo, hi, res):
@@ -147,26 +156,34 @@ def tile_list_tabres_bias_kernel(
 
         for c in range(S // CHUNK):
             gather_words(c)
-        h_first = keep.tile([P, CHUNK], U32, name="h_first", align_bytes=64)
-        res = keep.tile([P, S], F32, name="res", align_bytes=64)
+        res = keep.tile([P, S // 2], F32, name="res", align_bytes=64)
+        y_out = [keep.tile([P, CHUNK], F32, name=f"y_out{c}", align_bytes=64) for c in range(2)]
         first_product(0)
-        plane_first = keep.tile([P, CHUNK], U8, name="plane_first", align_bytes=64)
-        second_product(0, 512, h_first[:], plane_first[:], 4)
+        quantise_h(0, 512)
+        open_bank(0, 4)
+        second_product(0, 512)
         first_product(1)
-        gather_residual(res[:, :512], 0, 512)
-        y_first = keep.tile([P, CHUNK], F32, name="y_first", align_bytes=64)
-        finish_aside(0, 512, y_first[:], res[:, :512])
+        gather_residual(res[:], 1024, 2048)
+        bring_out(0, 512, y_out[0][:])
+        quantise_h(512, 1024)
+        open_bank(512, 5)
+        second_product(512, 1024)
+        finish_fused(0, 512, y_out[0][:])
         first_product(2)
+        bring_out(512, 1024, y_out[1][:])
         first_product(3)
-        gather_residual(res[:, 512:], 512, 2048)
-        h_rest = keep.tile([P, S - CHUNK], U32, name="h_rest", align_bytes=64)
-        plane_rest = keep.tile([P, S - CHUNK], U8, name="plane_rest", tag="words3", align_bytes=64)
-        second_product(512, 1024, h_rest[:, :512], plane_rest[:, :512], 5)
-        second_product(1024, 1536, h_rest[:, 512:1024], plane_rest[:, 512:1024], H_BANKS - 1)
-        second_product(1536, 1792, h_rest[:, 1024:1280], plane_rest[:, 1024:1280], 6)
-        second_product(1792, 2048, h_rest[:, 1280:], plane_rest[:, 1280:], 7)
-        finish(512, 1024, res[:, 512:1024])
-        finish(1024, 1280, res[:, 1024:1280])
-        finish(1280, 1536, res[:, 1280:1536])
-        finish(1536, 1792, res[:, 1536:1792])
-        finish(1792, 2048, res[:, 1792:])
+        quantise_h(1024, 1536)
+        finish_fused(512, 1024, y_out[1][:])
+        quantise_h(1536, 1792)
+        open_bank(1024, 1)
+        second_product(1024, 1536)
+        finish(1024, 1536, res[:, :512])
+        quantise_h(1792, 1920)
+        quantise_h(1920, 2048)
+        open_bank(1536, 3)
+        second_product(1536, 1792)
+        open_bank(1792, 6)
+        second_product(1792, 1920)
+        second_product(1920, 2048)
+        finish(1536, 1792, res[:, 512:768])
+        finish(1792, 2048, res[:, 768:])

@@ -23,7 +23,6 @@ LANES = 16
 CHUNK = 512
 SUB = 128
 SCALE_ROW0 = 112
-RES_HEAD = 512
 H_BANKS = 4
 
 
@@ -59,17 +58,16 @@ def tile_list_tabres_bias_kernel(
         w2_codes = keep.tile([P, 2 * M // 4], I32, name="w2_codes", align_bytes=64)
         nc.sync.dma_start(w2_codes[:], w2_words[0].bitcast(I32))
 
-        res_win = keep.tile([P, T], F32, name="res_win", align_bytes=64)
-        nc.sync.dma_start(res_win[:, :RES_HEAD], rT[:, :RES_HEAD])
+        bias = keep.tile([P, 1], F32, name="bias", align_bytes=64)
+        nc.sync.dma_start(bias[:], b.rearrange("(p o) -> p o", o=1))
 
         picked_scales = keep.tile([P, S], U8, name="picked_scales", align_bytes=64)
         nc.vector.tensor_copy(picked_scales[:], scale_win[:].bitcast(U8).indirect(picks(0, S)))
         for r in range(4):
             nc.sync.dma_start(tok_plane[r:P:32, :], picked_scales[:].bitcast(I32)[SCALE_ROW0 + r : P : 4, :])
         tok_scales = tok_plane[:].bitcast(U8)
-        nc.sync.dma_start(res_win[:, RES_HEAD:], rT[:, RES_HEAD:])
-        bias = keep.tile([P, 1], F32, name="bias", align_bytes=64)
-        nc.sync.dma_start(bias[:], b.rearrange("(p o) -> p o", o=1))
+        res_win = keep.tile([P, T], F32, name="res_win", align_bytes=64)
+        nc.sync.dma_start(res_win[:], rT)
 
         w1_bf = keep.tile([P, H * PACK], BF16, name="w1_bf", align_bytes=64)
         nc.scalar.copy(
@@ -114,13 +112,17 @@ def tile_list_tabres_bias_kernel(
                 )
 
         h_codes = keep.tile([P, S], U32, name="h_codes", align_bytes=64)
-        h_plane = keep.tile([P, S], U8, name="h_plane", align_bytes=64)
+        h_planes = {}
+
+        def plane_of(lo, hi):
+            base = max(k for k in h_planes if k <= lo)
+            return h_planes[base][:, lo - base : hi - base]
 
         def quantise_h(lo, hi):
             base = lo % CHUNK
             nc.vector.quantize_mx(
                 out=h_codes[:, lo:hi].bitcast(FP8X4),
-                scales=h_plane[:, lo:hi],
+                scales=plane_of(lo, hi),
                 in_=h_bf[lo // CHUNK][:, base * PACK : (base + hi - lo) * PACK],
             )
 
@@ -134,7 +136,7 @@ def tile_list_tabres_bias_kernel(
                 lhsT=w2_codes[:].bitcast(U8).bitcast(FP4X4),
                 lhsT_scale=w2_plane[:].bitcast(U8),
                 rhs=h_codes[:, lo:hi].bitcast(FP8X4),
-                rhs_scale=h_plane[:, lo:hi],
+                rhs_scale=plane_of(lo, hi),
                 start=True,
                 stop=True,
             )
@@ -158,6 +160,8 @@ def tile_list_tabres_bias_kernel(
             gather_words(c)
         res = keep.tile([P, S // 2], F32, name="res", align_bytes=64)
         y_out = [keep.tile([P, CHUNK], F32, name=f"y_out{c}", align_bytes=64) for c in range(2)]
+        h_planes[0] = keep.tile([P, CHUNK], U8, name="plane_first", align_bytes=64)
+        h_planes[1024] = keep.tile([P, S // 2], U8, name="plane_rest", align_bytes=64)
         first_product(0)
         quantise_h(0, 512)
         open_bank(0, 4)
@@ -165,11 +169,12 @@ def tile_list_tabres_bias_kernel(
         first_product(1)
         gather_residual(res[:], 1024, 2048)
         bring_out(0, 512, y_out[0][:])
+        first_product(2)
+        h_planes[512] = keep.tile([P, CHUNK], U8, name="plane_second", tag="words2", align_bytes=64)
         quantise_h(512, 1024)
         open_bank(512, 5)
         second_product(512, 1024)
         finish_fused(0, 512, y_out[0][:])
-        first_product(2)
         bring_out(512, 1024, y_out[1][:])
         first_product(3)
         quantise_h(1024, 1536)

@@ -90,10 +90,11 @@ def tile_list_tabres_bias_kernel(
         def gather_words(c):
             nc.vector.tensor_copy(tok_words[c][:], word_win[:].bitcast(U32).indirect(picks(c * CHUNK, (c + 1) * CHUNK)))
 
-        def first_product(c):
-            for s0 in range(0, CHUNK, SUB):
+        def first_product(c, first=0):
+            for turn in range(CHUNK // SUB):
+                s0 = (first + turn * SUB) % CHUNK
                 cols = slice(c * CHUNK + s0, c * CHUNK + s0 + SUB)
-                bank = psum.tile([P, PACK, SUB], F32, name="h_bank", tag=f"bank{cols.start // SUB % H_BANKS}")
+                bank = psum.tile([P, PACK, SUB], F32, name="h_bank", tag=f"bank{turn % H_BANKS}")
                 for t in range(PACK):
                     ch = slice(t * P, (t + 1) * P)
                     nc.tensor.matmul_mx(
@@ -159,7 +160,7 @@ def tile_list_tabres_bias_kernel(
         for c in range(S // CHUNK):
             gather_words(c)
         res = keep.tile([P, S // 2], F32, name="res", align_bytes=64)
-        y_out = [keep.tile([P, CHUNK], F32, name=f"y_out{c}", align_bytes=64) for c in range(2)]
+        y_out = [keep.tile([P, CHUNK], F32, name=f"y_out{c}", align_bytes=64) for c in range(3)]
         h_planes[0] = keep.tile([P, CHUNK], U8, name="plane_first", align_bytes=64)
         h_planes[1024] = keep.tile([P, S // 2], U8, name="plane_rest", align_bytes=64)
         first_product(0)
@@ -167,28 +168,32 @@ def tile_list_tabres_bias_kernel(
         open_bank(0, 4)
         second_product(0, 512)
         first_product(1)
-        gather_residual(res[:], 1024, 2048)
+        gather_residual(res[:], 768, 1792)
         bring_out(0, 512, y_out[0][:])
         first_product(2)
         h_planes[512] = keep.tile([P, CHUNK], U8, name="plane_second", tag="words2", align_bytes=64)
         quantise_h(512, 1024)
         open_bank(512, 5)
-        second_product(512, 1024)
+        second_product(512, 768)
+        open_bank(768, 7)
+        second_product(768, 1024)
         finish_fused(0, 512, y_out[0][:])
-        bring_out(512, 1024, y_out[1][:])
-        first_product(3)
+        bring_out(512, 768, y_out[1][:, :256])
+        finish(768, 1024, res[:, :256])
+        first_product(3, first=256)
         quantise_h(1024, 1536)
-        finish_fused(512, 1024, y_out[1][:])
-        quantise_h(1536, 1792)
+        finish_fused(512, 768, y_out[1][:, :256])
+        quantise_h(1792, 2048)
         open_bank(1024, 1)
         second_product(1024, 1536)
-        finish(1024, 1536, res[:, :512])
-        quantise_h(1792, 1920)
-        quantise_h(1920, 2048)
-        open_bank(1536, 3)
-        second_product(1536, 1792)
         open_bank(1792, 6)
-        second_product(1792, 1920)
-        second_product(1920, 2048)
-        finish(1536, 1792, res[:, 512:768])
-        finish(1792, 2048, res[:, 768:])
+        second_product(1792, 2048)
+        finish(1024, 1536, res[:, 256:768])
+        quantise_h(1536, 1664)
+        quantise_h(1664, 1792)
+        bring_out(1792, 2048, y_out[2][:, :256])
+        open_bank(1536, 4)
+        second_product(1536, 1664)
+        second_product(1664, 1792)
+        finish_fused(1792, 2048, y_out[2][:, :256])
+        finish(1536, 1792, res[:, 768:])

@@ -24,6 +24,7 @@ CHUNK = 512
 SUB = 128
 SCALE_ROW0 = 112
 H_BANKS = 4
+STORE = 256
 
 
 def tile_list_tabres_bias_kernel(
@@ -148,14 +149,19 @@ def tile_list_tabres_bias_kernel(
         def bring_out(lo, hi, y_biased):
             nc.scalar.activation(y_biased, y_banks[lo][:, : hi - lo], IDENTITY, bias=bias[:])
 
+        def store(lo, hi):
+            for s0 in range(lo, hi, STORE):
+                cols = slice(s0, min(s0 + STORE, hi))
+                nc.sync.dma_start(out[:, cols], total[:, cols])
+
         def finish_fused(lo, hi, y_biased):
             nc.vector.tensor_tensor(total[:, lo:hi], res_win[:].indirect(picks(lo, hi)), y_biased, ADD)
-            nc.sync.dma_start(out[:, lo:hi], total[:, lo:hi])
+            store(lo, hi)
 
         def finish(lo, hi, res):
             base = max(k for k in y_banks if k <= lo)
             nc.vector.scalar_tensor_tensor(total[:, lo:hi], y_banks[base][:, lo - base : hi - base], bias[:], res, ADD, ADD)
-            nc.sync.dma_start(out[:, lo:hi], total[:, lo:hi])
+            store(lo, hi)
 
         for c in range(S // CHUNK):
             gather_words(c)
@@ -196,4 +202,5 @@ def tile_list_tabres_bias_kernel(
         second_product(1536, 1664)
         second_product(1664, 1792)
         finish_fused(1792, 2048, y_out[2][:, :256])
-        finish(1536, 1792, res[:, 768:])
+        finish(1536, 1664, res[:, 768:896])
+        finish(1664, 1792, res[:, 896:])

@@ -79,20 +79,21 @@ def tile_list_tabres_bias_kernel(
         w1_plane = keep.tile([P, H], U8, name="w1_plane", align_bytes=64)
         nc.vector.quantize_mx(out=w1_codes[:].bitcast(FP8X4), scales=w1_plane[:], in_=w1_bf[:])
 
-        tok_words = [
-            keep.tile([P, CHUNK], U32, name=f"tok_words{c}", tag=f"words{c}", align_bytes=64) for c in range(S // CHUNK)
-        ]
+        first_words = keep.tile([P, CHUNK], U32, name="first_words", align_bytes=64)
+        middle_words = keep.tile([P, 2 * CHUNK], U32, name="middle_words", tag="words2", align_bytes=64)
+        last_words = keep.tile([P, CHUNK], U32, name="last_words", align_bytes=64)
+        tok_words = [first_words[:], middle_words[:, :CHUNK], middle_words[:, CHUNK:], last_words[:]]
         h_bf = [
             keep.tile([P, CHUNK * PACK], BF16, name=f"h_bf{c}", tag=f"h{c}", align_bytes=64) for c in range(S // CHUNK)
         ]
         total = keep.tile([P, S], F32, name="total", align_bytes=64)
         y_banks = {}
 
-        def gather_words(c):
-            nc.vector.tensor_copy(tok_words[c][:], word_win[:].bitcast(U32).indirect(picks(c * CHUNK, (c + 1) * CHUNK)))
+        def gather_words(dst, lo, hi):
+            nc.vector.tensor_copy(dst[:], word_win[:].bitcast(U32).indirect(picks(lo, hi)))
 
-        def first_product(c, first=0):
-            for turn in range(CHUNK // SUB):
+        def first_product(c, first=0, turns=range(CHUNK // SUB)):
+            for turn in turns:
                 s0 = (first + turn * SUB) % CHUNK
                 cols = slice(c * CHUNK + s0, c * CHUNK + s0 + SUB)
                 bank = psum.tile([P, PACK, SUB], F32, name="h_bank", tag=f"bank{turn % H_BANKS}")
@@ -150,8 +151,9 @@ def tile_list_tabres_bias_kernel(
             nc.scalar.activation(y_biased, y_banks[lo][:, : hi - lo], IDENTITY, bias=bias[:])
 
         def store(lo, hi):
-            for s0 in range(lo, hi, STORE):
-                cols = slice(s0, min(s0 + STORE, hi))
+            width = 384 if lo == 640 else STORE
+            for s0 in range(lo, hi, width):
+                cols = slice(s0, min(s0 + width, hi))
                 nc.sync.dma_start(out[:, cols], total[:, cols])
 
         def finish_fused(lo, hi, y_biased):
@@ -163,9 +165,10 @@ def tile_list_tabres_bias_kernel(
             nc.vector.scalar_tensor_tensor(total[:, lo:hi], y_banks[base][:, lo - base : hi - base], bias[:], res, ADD, ADD)
             store(lo, hi)
 
-        for c in range(S // CHUNK):
-            gather_words(c)
-        res = keep.tile([P, S // 2], F32, name="res", align_bytes=64)
+        gather_words(first_words, 0, 512)
+        gather_words(middle_words, 512, 1536)
+        gather_words(last_words, 1536, 2048)
+        res = keep.tile([P, 1152], F32, name="res", align_bytes=64)
         y_out = [keep.tile([P, CHUNK], F32, name=f"y_out{c}", align_bytes=64) for c in range(3)]
         h_planes[0] = keep.tile([P, CHUNK], U8, name="plane_first", align_bytes=64)
         h_planes[1024] = keep.tile([P, S // 2], U8, name="plane_rest", align_bytes=64)
@@ -174,27 +177,29 @@ def tile_list_tabres_bias_kernel(
         open_bank(0, 4)
         second_product(0, 512)
         first_product(1)
-        gather_residual(res[:], 768, 1792)
+        gather_residual(res[:], 640, 1792)
         bring_out(0, 512, y_out[0][:])
         first_product(2)
         h_planes[512] = keep.tile([P, CHUNK], U8, name="plane_second", tag="words2", align_bytes=64)
         quantise_h(512, 1024)
         open_bank(512, 5)
-        second_product(512, 768)
-        open_bank(768, 7)
+        second_product(512, 640)
+        open_bank(640, 7)
+        second_product(640, 768)
         second_product(768, 1024)
         finish_fused(0, 512, y_out[0][:])
-        bring_out(512, 768, y_out[1][:, :256])
-        finish(768, 1024, res[:, :256])
-        first_product(3, first=256)
+        finish(640, 1024, res[:, :384])
+        first_product(3, first=256, turns=range(0, 2))
+        bring_out(512, 640, y_out[1][:, :128])
+        first_product(3, first=256, turns=range(2, 4))
         quantise_h(1024, 1536)
-        finish_fused(512, 768, y_out[1][:, :256])
         quantise_h(1792, 2048)
+        finish_fused(512, 640, y_out[1][:, :128])
         open_bank(1024, 1)
         second_product(1024, 1536)
         open_bank(1792, 6)
         second_product(1792, 2048)
-        finish(1024, 1536, res[:, 256:768])
+        finish(1024, 1536, res[:, 384:896])
         quantise_h(1536, 1664)
         quantise_h(1664, 1792)
         bring_out(1792, 2048, y_out[2][:, :256])
@@ -202,5 +207,5 @@ def tile_list_tabres_bias_kernel(
         second_product(1536, 1664)
         second_product(1664, 1792)
         finish_fused(1792, 2048, y_out[2][:, :256])
-        finish(1536, 1664, res[:, 768:896])
-        finish(1664, 1792, res[:, 896:])
+        finish(1536, 1664, res[:, 896:1024])
+        finish(1664, 1792, res[:, 1024:])

@@ -148,7 +148,8 @@ def tile_list_tabres_bias_kernel(
             nc.vector.tensor_copy(dst, res_win[:].indirect(picks(lo, hi)))
 
         def bring_out(lo, hi, y_biased):
-            nc.scalar.activation(y_biased, y_banks[lo][:, : hi - lo], IDENTITY, bias=bias[:])
+            base = max(k for k in y_banks if k <= lo)
+            nc.scalar.activation(y_biased, y_banks[base][:, lo - base : hi - base], IDENTITY, bias=bias[:])
 
         def store(lo, hi):
             width = 384 if lo == 640 else STORE
@@ -168,7 +169,7 @@ def tile_list_tabres_bias_kernel(
         gather_words(first_words, 0, 512)
         gather_words(middle_words, 512, 1536)
         gather_words(last_words, 1536, 2048)
-        res = keep.tile([P, 1152], F32, name="res", align_bytes=64)
+        res = keep.tile([P, 1024], F32, name="res", align_bytes=64)
         y_out = [keep.tile([P, CHUNK], F32, name=f"y_out{c}", align_bytes=64) for c in range(3)]
         h_planes[0] = keep.tile([P, CHUNK], U8, name="plane_first", align_bytes=64)
         h_planes[1024] = keep.tile([P, S // 2], U8, name="plane_rest", align_bytes=64)
@@ -177,7 +178,7 @@ def tile_list_tabres_bias_kernel(
         open_bank(0, 4)
         second_product(0, 512)
         first_product(1)
-        gather_residual(res[:], 640, 1792)
+        gather_residual(res[:], 640, 1664)
         bring_out(0, 512, y_out[0][:])
         first_product(2)
         h_planes[512] = keep.tile([P, CHUNK], U8, name="plane_second", tag="words2", align_bytes=64)
@@ -189,23 +190,26 @@ def tile_list_tabres_bias_kernel(
         second_product(768, 1024)
         finish_fused(0, 512, y_out[0][:])
         finish(640, 1024, res[:, :384])
-        first_product(3, first=256, turns=range(0, 2))
+        first_product(3, first=128, turns=range(0, 2))
         bring_out(512, 640, y_out[1][:, :128])
-        first_product(3, first=256, turns=range(2, 4))
+        first_product(3, first=128, turns=range(2, 4))
         quantise_h(1024, 1536)
-        quantise_h(1792, 2048)
+        quantise_h(1664, 1920)
         finish_fused(512, 640, y_out[1][:, :128])
         open_bank(1024, 1)
         second_product(1024, 1536)
-        open_bank(1792, 6)
-        second_product(1792, 2048)
-        finish(1024, 1536, res[:, 384:896])
+        open_bank(1664, 6)
+        second_product(1664, 1920)
+        finish(1024, 1280, res[:, 384:640])
+        quantise_h(1920, 2048)
+        finish(1280, 1536, res[:, 640:896])
         quantise_h(1536, 1664)
-        quantise_h(1664, 1792)
-        bring_out(1792, 2048, y_out[2][:, :256])
-        open_bank(1536, 4)
+        open_bank(1920, 4)
+        second_product(1920, 2048)
+        open_bank(1536, 5)
         second_product(1536, 1664)
-        second_product(1664, 1792)
-        finish_fused(1792, 2048, y_out[2][:, :256])
+        bring_out(1664, 1920, y_out[2][:, :256])
+        bring_out(1920, 2048, y_out[2][:, 256:384])
+        finish_fused(1664, 1920, y_out[2][:, :256])
+        finish_fused(1920, 2048, y_out[2][:, 256:384])
         finish(1536, 1664, res[:, 896:1024])
-        finish(1664, 1792, res[:, 1024:])

@@ -35,7 +35,7 @@ def tile_list_tabres_bias_kernel(
         keep = ctx.enter_context(tc.tile_pool(name="keep", bufs=1))
         psum = ctx.enter_context(tc.psum_pool(name="psum", bufs=1))
 
-        scale_win = keep.tile([P, T // 4], I32, name="scale_win", align_bytes=64)
+        scale_win = keep.tile([P, T // 4], I32, name="scale_win", align_bytes=256)
         nc.sync.dma_start(scale_win[SCALE_ROW0:P, :], tab_scales[0].bitcast(I32))
         offsets = keep.tile([P, S // LANES], U16, name="offsets")
         nc.sync.dma_start(offsets[:], offs)
@@ -43,50 +43,50 @@ def tile_list_tabres_bias_kernel(
         def picks(lo, hi):
             return offsets[:, lo // LANES : hi // LANES]
 
-        w2_plane = keep.tile([P, M // 4], I32, name="w2_plane", align_bytes=64)
+        w2_plane = keep.tile([P, M // 4], I32, name="w2_plane", align_bytes=256)
         nc.vector.memset(w2_plane[:], 0)
         nc.vector.memset(scale_win[0:SCALE_ROW0, :], 0)
-        tok_plane = keep.tile([P, S // 4], I32, name="tok_plane", align_bytes=64)
+        tok_plane = keep.tile([P, S // 4], I32, name="tok_plane", align_bytes=256)
         nc.vector.memset(tok_plane[:], 0)
 
-        w1_raw = keep.tile([P, PACK, H], F32, name="w1_raw", align_bytes=64)
+        w1_raw = keep.tile([P, PACK, H], F32, name="w1_raw", align_bytes=256)
         nc.sync.dma_start(w1_raw[:], w1.rearrange("(p j) r -> p j r", j=PACK))
         w2_scale_rows = w2_scales[0].bitcast(I32)
         for r in range(4):
             nc.sync.dma_start(w2_plane[r:P:32, :], w2_scale_rows[r:16:4, :])
-        word_win = keep.tile([P, T], I32, name="word_win", align_bytes=64)
+        word_win = keep.tile([P, T], I32, name="word_win", align_bytes=256)
         nc.sync.dma_start(word_win[:], tab_words[0].rearrange("p t i -> p (t i)").bitcast(I32))
-        w2_codes = keep.tile([P, 2 * M // 4], I32, name="w2_codes", align_bytes=64)
+        w2_codes = keep.tile([P, 2 * M // 4], I32, name="w2_codes", align_bytes=256)
         nc.sync.dma_start(w2_codes[:], w2_words[0].bitcast(I32))
 
-        bias = keep.tile([P, 1], F32, name="bias", align_bytes=64)
+        bias = keep.tile([P, 1], F32, name="bias", align_bytes=256)
         nc.sync.dma_start(bias[:], b.rearrange("(p o) -> p o", o=1))
 
-        picked_scales = keep.tile([P, S], U8, name="picked_scales", align_bytes=64)
+        picked_scales = keep.tile([P, S], U8, name="picked_scales", align_bytes=256)
         nc.vector.tensor_copy(picked_scales[:], scale_win[:].bitcast(U8).indirect(picks(0, S)))
         for r in range(4):
             nc.sync.dma_start(tok_plane[r:P:32, :], picked_scales[:].bitcast(I32)[SCALE_ROW0 + r : P : 4, :])
         tok_scales = tok_plane[:].bitcast(U8)
-        res_win = keep.tile([P, T], F32, name="res_win", align_bytes=64)
+        res_win = keep.tile([P, T], F32, name="res_win", align_bytes=256)
         nc.sync.dma_start(res_win[:], rT)
 
-        w1_bf = keep.tile([P, H * PACK], BF16, name="w1_bf", align_bytes=64)
+        w1_bf = keep.tile([P, H * PACK], BF16, name="w1_bf", align_bytes=256)
         nc.scalar.copy(
             w1_bf[:].rearrange("p (t m j) -> p m t j", t=PACK, j=PACK),
             w1_raw[:].rearrange("p j (m t) -> p m t j", t=PACK),
         )
-        w1_codes = keep.tile([P, H], U32, name="w1_codes", align_bytes=64)
-        w1_plane = keep.tile([P, H], U8, name="w1_plane", align_bytes=64)
+        w1_codes = keep.tile([P, H], U32, name="w1_codes", align_bytes=256)
+        w1_plane = keep.tile([P, H], U8, name="w1_plane", align_bytes=256)
         nc.vector.quantize_mx(out=w1_codes[:].bitcast(FP8X4), scales=w1_plane[:], in_=w1_bf[:])
 
-        first_words = keep.tile([P, CHUNK], U32, name="first_words", align_bytes=64)
-        middle_words = keep.tile([P, 2 * CHUNK], U32, name="middle_words", tag="words2", align_bytes=64)
-        last_words = keep.tile([P, CHUNK], U32, name="last_words", align_bytes=64)
+        first_words = keep.tile([P, CHUNK], U32, name="first_words", align_bytes=256)
+        middle_words = keep.tile([P, 2 * CHUNK], U32, name="middle_words", tag="words2", align_bytes=256)
+        last_words = keep.tile([P, CHUNK], U32, name="last_words", align_bytes=256)
         tok_words = [first_words[:], middle_words[:, :CHUNK], middle_words[:, CHUNK:], last_words[:]]
         h_bf = [
-            keep.tile([P, CHUNK * PACK], BF16, name=f"h_bf{c}", tag=f"h{c}", align_bytes=64) for c in range(S // CHUNK)
+            keep.tile([P, CHUNK * PACK], BF16, name=f"h_bf{c}", tag=f"h{c}", align_bytes=256) for c in range(S // CHUNK)
         ]
-        total = keep.tile([P, S], F32, name="total", align_bytes=64)
+        total = keep.tile([P, S], F32, name="total", align_bytes=256)
         y_banks = {}
 
         def gather_words(dst, lo, hi):
@@ -114,7 +114,7 @@ def tile_list_tabres_bias_kernel(
                     RELU,
                 )
 
-        h_codes = keep.tile([P, S], U32, name="h_codes", align_bytes=64)
+        h_codes = keep.tile([P, S], U32, name="h_codes", align_bytes=256)
         h_planes = {}
 
         def plane_of(lo, hi):
@@ -169,10 +169,10 @@ def tile_list_tabres_bias_kernel(
         gather_words(first_words, 0, 512)
         gather_words(middle_words, 512, 1536)
         gather_words(last_words, 1536, 2048)
-        res = keep.tile([P, 1024], F32, name="res", align_bytes=64)
-        y_out = [keep.tile([P, CHUNK], F32, name=f"y_out{c}", align_bytes=64) for c in range(3)]
-        h_planes[0] = keep.tile([P, CHUNK], U8, name="plane_first", align_bytes=64)
-        h_planes[1024] = keep.tile([P, S // 2], U8, name="plane_rest", align_bytes=64)
+        res = keep.tile([P, 1024], F32, name="res", align_bytes=256)
+        y_out = [keep.tile([P, CHUNK], F32, name=f"y_out{c}", align_bytes=256) for c in range(3)]
+        h_planes[0] = keep.tile([P, CHUNK], U8, name="plane_first", align_bytes=256)
+        h_planes[1024] = keep.tile([P, S // 2], U8, name="plane_rest", align_bytes=256)
         first_product(0)
         quantise_h(0, 512)
         open_bank(0, 4)
@@ -181,7 +181,7 @@ def tile_list_tabres_bias_kernel(
         gather_residual(res[:], 640, 1664)
         bring_out(0, 512, y_out[0][:])
         first_product(2)
-        h_planes[512] = keep.tile([P, CHUNK], U8, name="plane_second", tag="words2", align_bytes=64)
+        h_planes[512] = keep.tile([P, CHUNK], U8, name="plane_second", tag="words2", align_bytes=256)
         quantise_h(512, 1024)
         open_bank(512, 5)
         second_product(512, 640)

@@ -24,7 +24,7 @@ CHUNK = 512
 SUB = 128
 SCALE_ROW0 = 112
 H_BANKS = 4
-STORE = 256
+ALIGN = 256
 
 
 def tile_list_tabres_bias_kernel(
@@ -33,9 +33,11 @@ def tile_list_tabres_bias_kernel(
     nc = tc.nc
     with ExitStack() as ctx:
         keep = ctx.enter_context(tc.tile_pool(name="keep", bufs=1))
+        shared = ctx.enter_context(tc.tile_pool(name="shared", bufs=1))
         psum = ctx.enter_context(tc.psum_pool(name="psum", bufs=1))
 
-        scale_win = keep.tile([P, T // 4], I32, name="scale_win", align_bytes=256)
+        res_bytes = T * 4
+        scale_win = shared.tile([P, T // 4], I32, name="scale_win", offset=res_bytes - ALIGN, align_bytes=ALIGN)
         nc.sync.dma_start(scale_win[SCALE_ROW0:P, :], tab_scales[0].bitcast(I32))
         offsets = keep.tile([P, S // LANES], U16, name="offsets")
         nc.sync.dma_start(offsets[:], offs)
@@ -43,173 +45,167 @@ def tile_list_tabres_bias_kernel(
         def picks(lo, hi):
             return offsets[:, lo // LANES : hi // LANES]
 
-        w2_plane = keep.tile([P, M // 4], I32, name="w2_plane", align_bytes=256)
+        w2_plane = keep.tile([P, M // 4], I32, name="w2_plane", align_bytes=ALIGN)
         nc.vector.memset(w2_plane[:], 0)
         nc.vector.memset(scale_win[0:SCALE_ROW0, :], 0)
-        tok_plane = keep.tile([P, S // 4], I32, name="tok_plane", align_bytes=256)
+        tok_plane = keep.tile([P, S // 4], I32, name="tok_plane", align_bytes=ALIGN)
         nc.vector.memset(tok_plane[:], 0)
 
-        w1_raw = keep.tile([P, PACK, H], F32, name="w1_raw", align_bytes=256)
+        w1_raw = keep.tile([P, PACK, H], F32, name="w1_raw", align_bytes=ALIGN)
         nc.sync.dma_start(w1_raw[:], w1.rearrange("(p j) r -> p j r", j=PACK))
         w2_scale_rows = w2_scales[0].bitcast(I32)
         for r in range(4):
             nc.sync.dma_start(w2_plane[r:P:32, :], w2_scale_rows[r:16:4, :])
-        word_win = keep.tile([P, T], I32, name="word_win", align_bytes=256)
+        word_win = keep.tile([P, T], I32, name="word_win", align_bytes=ALIGN)
         nc.sync.dma_start(word_win[:], tab_words[0].rearrange("p t i -> p (t i)").bitcast(I32))
-        w2_codes = keep.tile([P, 2 * M // 4], I32, name="w2_codes", align_bytes=256)
+        w2_codes = keep.tile([P, 2 * M // 4], I32, name="w2_codes", align_bytes=ALIGN)
         nc.sync.dma_start(w2_codes[:], w2_words[0].bitcast(I32))
-
-        bias = keep.tile([P, 1], F32, name="bias", align_bytes=256)
+        bias = keep.tile([P, 1], F32, name="bias", align_bytes=ALIGN)
         nc.sync.dma_start(bias[:], b.rearrange("(p o) -> p o", o=1))
 
-        picked_scales = keep.tile([P, S], U8, name="picked_scales", align_bytes=256)
+        picked_scales = keep.tile([P, S], U8, name="picked_scales", align_bytes=ALIGN)
         nc.vector.tensor_copy(picked_scales[:], scale_win[:].bitcast(U8).indirect(picks(0, S)))
         for r in range(4):
             nc.sync.dma_start(tok_plane[r:P:32, :], picked_scales[:].bitcast(I32)[SCALE_ROW0 + r : P : 4, :])
         tok_scales = tok_plane[:].bitcast(U8)
-        res_win = keep.tile([P, T], F32, name="res_win", align_bytes=256)
+
+        res_win = shared.tile([P, T], F32, name="res_win", offset=0, align_bytes=ALIGN)
         nc.sync.dma_start(res_win[:], rT)
 
-        w1_bf = keep.tile([P, H * PACK], BF16, name="w1_bf", align_bytes=256)
+        w1_bf = keep.tile([P, H * PACK], BF16, name="w1_bf", align_bytes=ALIGN)
         nc.scalar.copy(
             w1_bf[:].rearrange("p (t m j) -> p m t j", t=PACK, j=PACK),
             w1_raw[:].rearrange("p j (m t) -> p m t j", t=PACK),
         )
-        w1_codes = keep.tile([P, H], U32, name="w1_codes", align_bytes=256)
-        w1_plane = keep.tile([P, H], U8, name="w1_plane", align_bytes=256)
+        w1_codes = keep.tile([P, H], U32, name="w1_codes", align_bytes=ALIGN)
+        w1_plane = keep.tile([P, H], U8, name="w1_plane", align_bytes=ALIGN)
         nc.vector.quantize_mx(out=w1_codes[:].bitcast(FP8X4), scales=w1_plane[:], in_=w1_bf[:])
 
-        first_words = keep.tile([P, CHUNK], U32, name="first_words", align_bytes=256)
-        middle_words = keep.tile([P, 2 * CHUNK], U32, name="middle_words", tag="words2", align_bytes=256)
-        last_words = keep.tile([P, CHUNK], U32, name="last_words", align_bytes=256)
-        tok_words = [first_words[:], middle_words[:, :CHUNK], middle_words[:, CHUNK:], last_words[:]]
-        h_bf = [
-            keep.tile([P, CHUNK * PACK], BF16, name=f"h_bf{c}", tag=f"h{c}", align_bytes=256) for c in range(S // CHUNK)
-        ]
-        total = keep.tile([P, S], F32, name="total", align_bytes=256)
+        words = {}
+        h_banks = {}
+        h_bf = {c: keep.tile([P, CHUNK * PACK], BF16, name=f"h_bf{c}", align_bytes=ALIGN) for c in range(0, S, CHUNK)}
+        h_codes = keep.tile([P, S], U32, name="h_codes", align_bytes=ALIGN)
+        planes = {}
         y_banks = {}
+        res = {}
+        y_out = keep.tile([P, S], F32, name="y_out", align_bytes=ALIGN)
+        total = keep.tile([P, S], F32, name="total", align_bytes=ALIGN)
 
-        def gather_words(dst, lo, hi):
-            nc.vector.tensor_copy(dst[:], word_win[:].bitcast(U32).indirect(picks(lo, hi)))
+        def part(tiles, lo, hi, width=1):
+            base = max(k for k in tiles if k <= lo)
+            return tiles[base][:, (lo - base) * width : (hi - base) * width]
 
-        def first_product(c, first=0, turns=range(CHUNK // SUB)):
-            for turn in turns:
-                s0 = (first + turn * SUB) % CHUNK
-                cols = slice(c * CHUNK + s0, c * CHUNK + s0 + SUB)
-                bank = psum.tile([P, PACK, SUB], F32, name="h_bank", tag=f"bank{turn % H_BANKS}")
+        def gather_words(lo, hi, tag):
+            words[lo] = keep.tile([P, hi - lo], U32, name=f"words{lo}", tag=tag, align_bytes=ALIGN)
+            nc.vector.tensor_copy(words[lo][:], word_win[:].bitcast(U32).indirect(picks(lo, hi)))
+
+        def first_product(lo, hi):
+            for s0 in range(lo, hi, SUB):
+                h_banks[s0] = psum.tile([P, PACK, SUB], F32, name="h_bank", tag=f"bank{len(h_banks) % H_BANKS}")
                 for t in range(PACK):
                     ch = slice(t * P, (t + 1) * P)
                     nc.tensor.matmul_mx(
-                        out=bank[:, t, :],
+                        out=h_banks[s0][:, t, :],
                         lhsT=w1_codes[:, ch].bitcast(FP8X4),
                         lhsT_scale=w1_plane[:, ch],
-                        rhs=tok_words[c][:, s0 : s0 + SUB].bitcast(FP8X4),
-                        rhs_scale=tok_scales[:, cols],
+                        rhs=part(words, s0, s0 + SUB).bitcast(FP8X4),
+                        rhs_scale=tok_scales[:, s0 : s0 + SUB],
                         start=True,
                         stop=True,
                     )
+
+        def relu(lo, hi):
+            for s0 in range(lo, hi, SUB):
                 nc.scalar.activation(
-                    h_bf[c][:, s0 * PACK : (s0 + SUB) * PACK].rearrange("p (n t) -> p n t", t=PACK),
-                    bank[:].rearrange("p t n -> p n t"),
+                    part(h_bf, s0, s0 + SUB, PACK).rearrange("p (n t) -> p n t", t=PACK),
+                    h_banks[s0][:].rearrange("p t n -> p n t"),
                     RELU,
                 )
 
-        h_codes = keep.tile([P, S], U32, name="h_codes", align_bytes=256)
-        h_planes = {}
+        def make_h(lo, hi):
+            for s0 in range(lo, hi, SUB):
+                first_product(s0, s0 + SUB)
+                relu(s0, s0 + SUB)
 
-        def plane_of(lo, hi):
-            base = max(k for k in h_planes if k <= lo)
-            return h_planes[base][:, lo - base : hi - base]
-
-        def quantise_h(lo, hi):
-            base = lo % CHUNK
+        def quantise_h(lo, hi, plane_tag):
+            planes[lo] = keep.tile([P, hi - lo], U8, name=f"plane{lo}", tag=plane_tag, align_bytes=ALIGN)
             nc.vector.quantize_mx(
-                out=h_codes[:, lo:hi].bitcast(FP8X4),
-                scales=plane_of(lo, hi),
-                in_=h_bf[lo // CHUNK][:, base * PACK : (base + hi - lo) * PACK],
+                out=h_codes[:, lo:hi].bitcast(FP8X4), scales=planes[lo][:], in_=part(h_bf, lo, hi, PACK)
             )
 
-        def open_bank(lo, bank_no):
-            y_banks[lo] = psum.tile([P, CHUNK], F32, name=f"y_bank{lo}", tag=f"bank{bank_no}")
+        def open_bank(lo, hi, bank):
+            y_banks[lo] = psum.tile([P, hi - lo], F32, name=f"y_bank{lo}", tag=f"bank{bank}")
 
         def second_product(lo, hi):
-            base = max(k for k in y_banks if k <= lo)
             nc.tensor.matmul_mx(
-                out=y_banks[base][:, lo - base : hi - base],
+                out=part(y_banks, lo, hi),
                 lhsT=w2_codes[:].bitcast(U8).bitcast(FP4X4),
                 lhsT_scale=w2_plane[:].bitcast(U8),
                 rhs=h_codes[:, lo:hi].bitcast(FP8X4),
-                rhs_scale=plane_of(lo, hi),
+                rhs_scale=part(planes, lo, hi),
                 start=True,
                 stop=True,
             )
 
-        def gather_residual(dst, lo, hi):
-            nc.vector.tensor_copy(dst, res_win[:].indirect(picks(lo, hi)))
+        def make_y(lo, hi, bank):
+            open_bank(lo, hi, bank)
+            second_product(lo, hi)
 
-        def bring_out(lo, hi, y_biased):
-            base = max(k for k in y_banks if k <= lo)
-            nc.scalar.activation(y_biased, y_banks[base][:, lo - base : hi - base], IDENTITY, bias=bias[:])
+        def gather_residual(lo, hi):
+            res[lo] = keep.tile([P, hi - lo], F32, name=f"res{lo}", align_bytes=ALIGN)
+            nc.vector.tensor_copy(res[lo][:], res_win[:].indirect(picks(lo, hi)))
 
-        def store(lo, hi):
-            width = 384 if lo == 640 else STORE
+        def bring_out(lo, hi):
+            nc.scalar.activation(y_out[:, lo:hi], part(y_banks, lo, hi), IDENTITY, bias=bias[:])
+
+        def store(lo, hi, pieces):
+            width = (hi - lo) // pieces
             for s0 in range(lo, hi, width):
-                cols = slice(s0, min(s0 + width, hi))
-                nc.sync.dma_start(out[:, cols], total[:, cols])
+                nc.sync.dma_start(out[:, s0 : s0 + width], total[:, s0 : s0 + width])
 
-        def finish_fused(lo, hi, y_biased):
-            nc.vector.tensor_tensor(total[:, lo:hi], res_win[:].indirect(picks(lo, hi)), y_biased, ADD)
-            store(lo, hi)
+        def sum_in_gather(lo, hi, pieces=1):
+            nc.vector.tensor_tensor(total[:, lo:hi], res_win[:].indirect(picks(lo, hi)), y_out[:, lo:hi], ADD)
+            store(lo, hi, pieces)
 
-        def finish(lo, hi, res):
-            base = max(k for k in y_banks if k <= lo)
-            nc.vector.scalar_tensor_tensor(total[:, lo:hi], y_banks[base][:, lo - base : hi - base], bias[:], res, ADD, ADD)
-            store(lo, hi)
+        def sum_from_bank(lo, hi, pieces=1):
+            nc.vector.scalar_tensor_tensor(total[:, lo:hi], part(y_banks, lo, hi), bias[:], part(res, lo, hi), ADD, ADD)
+            store(lo, hi, pieces)
 
-        gather_words(first_words, 0, 512)
-        gather_words(middle_words, 512, 1536)
-        gather_words(last_words, 1536, 2048)
-        res = keep.tile([P, 1024], F32, name="res", align_bytes=256)
-        y_out = [keep.tile([P, CHUNK], F32, name=f"y_out{c}", align_bytes=256) for c in range(3)]
-        h_planes[0] = keep.tile([P, CHUNK], U8, name="plane_first", align_bytes=256)
-        h_planes[1024] = keep.tile([P, S // 2], U8, name="plane_rest", align_bytes=256)
-        first_product(0)
-        quantise_h(0, 512)
-        open_bank(0, 4)
-        second_product(0, 512)
-        first_product(1)
-        gather_residual(res[:], 640, 1664)
-        bring_out(0, 512, y_out[0][:])
-        first_product(2)
-        h_planes[512] = keep.tile([P, CHUNK], U8, name="plane_second", tag="words2", align_bytes=256)
-        quantise_h(512, 1024)
-        open_bank(512, 5)
-        second_product(512, 640)
-        open_bank(640, 7)
-        second_product(640, 768)
-        second_product(768, 1024)
-        finish_fused(0, 512, y_out[0][:])
-        finish(640, 1024, res[:, :384])
-        first_product(3, first=128, turns=range(0, 2))
-        bring_out(512, 640, y_out[1][:, :128])
-        first_product(3, first=128, turns=range(2, 4))
-        quantise_h(1024, 1536)
-        quantise_h(1664, 1920)
-        finish_fused(512, 640, y_out[1][:, :128])
-        open_bank(1024, 1)
-        second_product(1024, 1536)
-        open_bank(1664, 6)
-        second_product(1664, 1920)
-        finish(1024, 1280, res[:, 384:640])
-        quantise_h(1920, 2048)
-        finish(1280, 1536, res[:, 640:896])
-        quantise_h(1536, 1664)
-        open_bank(1920, 4)
-        second_product(1920, 2048)
-        open_bank(1536, 5)
-        second_product(1536, 1664)
-        bring_out(1664, 1920, y_out[2][:, :256])
-        bring_out(1920, 2048, y_out[2][:, 256:384])
-        finish_fused(1664, 1920, y_out[2][:, :256])
-        finish_fused(1920, 2048, y_out[2][:, 256:384])
-        finish(1536, 1664, res[:, 896:1024])
+        gather_words(0, 256, "words0")
+        gather_words(256, 768, "words1")
+        gather_words(768, 1536, "words2")
+        gather_words(1536, 2048, "words3")
+        make_h(0, 512)
+        quantise_h(0, 512, "plane0")
+        make_y(0, 512, 4)
+        gather_residual(896, 1664)
+        make_h(512, 1024)
+        bring_out(0, 512)
+        make_h(1024, 1536)
+        quantise_h(512, 1024, "words2")
+        open_bank(512, 896, 5)
+        second_product(512, 768)
+        second_product(768, 896)
+        make_y(896, 1024, 6)
+        sum_in_gather(0, 512, 2)
+        sum_from_bank(896, 1024)
+        bring_out(512, 896)
+        quantise_h(1024, 1536, "plane2")
+        sum_in_gather(512, 896)
+        make_h(1664, 1920)
+        quantise_h(1664, 1920, "plane3")
+        make_y(1024, 1536, 1)
+        make_y(1664, 1920, 6)
+        sum_from_bank(1024, 1280)
+        make_h(1920, 2048)
+        quantise_h(1920, 2048, "plane4")
+        make_y(1920, 2048, 5)
+        sum_from_bank(1280, 1536)
+        make_h(1536, 1664)
+        quantise_h(1536, 1664, "plane5")
+        make_y(1536, 1664, 7)
+        bring_out(1664, 1920)
+        bring_out(1920, 2048)
+        sum_in_gather(1664, 1920)
+        sum_in_gather(1920, 2048)
+        sum_from_bank(1536, 1664)

@@ -91,17 +91,22 @@ def tile_list_tabres_bias_kernel(
         y_out = keep.tile([P, S], F32, name="y_out", align_bytes=ALIGN)
         total = keep.tile([P, S], F32, name="total", align_bytes=ALIGN)
 
+        def new_tile(name, width, dtype, place):
+            if isinstance(place, int):
+                return shared.tile([P, width], dtype, name=name, offset=place, align_bytes=ALIGN)
+            return keep.tile([P, width], dtype, name=name, tag=place, align_bytes=ALIGN)
+
         def part(tiles, lo, hi, width=1):
             base = max(k for k in tiles if k <= lo)
             return tiles[base][:, (lo - base) * width : (hi - base) * width]
 
         def gather_words(lo, hi, tag):
-            words[lo] = keep.tile([P, hi - lo], U32, name=f"words{lo}", tag=tag, align_bytes=ALIGN)
+            words[lo] = new_tile(f"words{lo}", hi - lo, U32, tag)
             nc.vector.tensor_copy(words[lo][:], word_win[:].bitcast(U32).indirect(picks(lo, hi)))
 
-        def first_product(lo, hi):
+        def first_product(lo, hi, bank=None):
             for s0 in range(lo, hi, SUB):
-                h_banks[s0] = psum.tile([P, PACK, SUB], F32, name="h_bank", tag=f"bank{len(h_banks) % H_BANKS}")
+                h_banks[s0] = psum.tile([P, PACK, SUB], F32, name="h_bank", tag=f"bank{len(h_banks) % H_BANKS if bank is None else bank}")
                 for t in range(PACK):
                     ch = slice(t * P, (t + 1) * P)
                     nc.tensor.matmul_mx(
@@ -122,13 +127,13 @@ def tile_list_tabres_bias_kernel(
                     RELU,
                 )
 
-        def make_h(lo, hi):
+        def make_h(lo, hi, bank=None):
             for s0 in range(lo, hi, SUB):
-                first_product(s0, s0 + SUB)
+                first_product(s0, s0 + SUB, bank)
                 relu(s0, s0 + SUB)
 
         def quantise_h(lo, hi, plane_tag):
-            planes[lo] = keep.tile([P, hi - lo], U8, name=f"plane{lo}", tag=plane_tag, align_bytes=ALIGN)
+            planes[lo] = new_tile(f"plane{lo}", hi - lo, U8, plane_tag)
             nc.vector.quantize_mx(
                 out=h_codes[:, lo:hi].bitcast(FP8X4), scales=planes[lo][:], in_=part(h_bf, lo, hi, PACK)
             )
@@ -151,8 +156,8 @@ def tile_list_tabres_bias_kernel(
             open_bank(lo, hi, bank)
             second_product(lo, hi)
 
-        def gather_residual(lo, hi):
-            res[lo] = keep.tile([P, hi - lo], F32, name=f"res{lo}", align_bytes=ALIGN)
+        def gather_residual(lo, hi, place):
+            res[lo] = new_tile(f"res{lo}", hi - lo, F32, place)
             nc.vector.tensor_copy(res[lo][:], res_win[:].indirect(picks(lo, hi)))
 
         def bring_out(lo, hi):
@@ -167,6 +172,10 @@ def tile_list_tabres_bias_kernel(
             nc.vector.tensor_tensor(total[:, lo:hi], res_win[:].indirect(picks(lo, hi)), y_out[:, lo:hi], ADD)
             store(lo, hi, pieces)
 
+        def sum_on_gpsimd(lo, hi, pieces=1):
+            nc.gpsimd.tensor_tensor(total[:, lo:hi], y_out[:, lo:hi], part(res, lo, hi), ADD)
+            store(lo, hi, pieces)
+
         def sum_from_bank(lo, hi, pieces=1):
             nc.vector.scalar_tensor_tensor(total[:, lo:hi], part(y_banks, lo, hi), bias[:], part(res, lo, hi), ADD, ADD)
             store(lo, hi, pieces)
@@ -178,7 +187,7 @@ def tile_list_tabres_bias_kernel(
         make_h(0, 512)
         quantise_h(0, 512, "plane0")
         make_y(0, 512, 4)
-        gather_residual(896, 1664)
+        gather_residual(896, 1792, "res")
         make_h(512, 1024)
         bring_out(0, 512)
         make_h(1024, 1536)
@@ -192,20 +201,20 @@ def tile_list_tabres_bias_kernel(
         bring_out(512, 896)
         quantise_h(1024, 1536, "plane2")
         sum_in_gather(512, 896)
-        make_h(1664, 1920)
-        quantise_h(1664, 1920, "plane3")
-        make_y(1024, 1536, 1)
-        make_y(1664, 1920, 6)
+        make_h(1792, 2048)
+        quantise_h(1792, 2048, "plane3")
+        make_y(1024, 1280, 1)
+        make_y(1792, 2048, 6)
         sum_from_bank(1024, 1280)
-        make_h(1920, 2048)
-        quantise_h(1920, 2048, "plane4")
-        make_y(1920, 2048, 5)
+        make_h(1536, 1664, 3)
+        quantise_h(1536, 1664, "plane4")
+        make_y(1280, 1536, 3)
+        make_y(1536, 1664, 5)
         sum_from_bank(1280, 1536)
-        make_h(1536, 1664)
-        quantise_h(1536, 1664, "plane5")
-        make_y(1536, 1664, 7)
-        bring_out(1664, 1920)
-        bring_out(1920, 2048)
-        sum_in_gather(1664, 1920)
-        sum_in_gather(1920, 2048)
+        make_h(1664, 1792, 0)
+        quantise_h(1664, 1792, "plane5")
+        make_y(1664, 1792, 7)
+        bring_out(1792, 2048)
         sum_from_bank(1536, 1664)
+        sum_in_gather(1792, 2048)
+        sum_from_bank(1664, 1792)

@@ -187,11 +187,13 @@ def tile_list_tabres_bias_kernel(
         make_h(0, 512)
         quantise_h(0, 512, "plane0")
         make_y(0, 512, 4)
+        make_h(512, 768)
+        quantise_h(512, 768, "plane1")
         gather_residual(896, 1792, "res")
-        make_h(512, 1024)
+        make_h(768, 1024)
         bring_out(0, 512)
         make_h(1024, 1536)
-        quantise_h(512, 1024, "words2")
+        quantise_h(768, 1024, "words2")
         open_bank(512, 896, 5)
         second_product(512, 768)
         second_product(768, 896)

@@ -73,10 +73,10 @@ def tile_list_tabres_bias_kernel(
         nc.sync.dma_start(res_win[:], rT)
 
         w1_bf = keep.tile([P, H * PACK], BF16, name="w1_bf", align_bytes=ALIGN)
-        nc.scalar.copy(
-            w1_bf[:].rearrange("p (t m j) -> p m t j", t=PACK, j=PACK),
-            w1_raw[:].rearrange("p j (m t) -> p m t j", t=PACK),
-        )
+        cast_to = w1_bf[:].rearrange("p (t m j) -> p m t j", t=PACK, j=PACK)
+        cast_from = w1_raw[:].rearrange("p j (m t) -> p m t j", t=PACK)
+        nc.scalar.copy(cast_to[:, :96], cast_from[:, :96])
+        nc.vector.tensor_copy(cast_to[:, 96:], cast_from[:, 96:])
         w1_codes = keep.tile([P, H], U32, name="w1_codes", align_bytes=ALIGN)
         w1_plane = keep.tile([P, H], U8, name="w1_plane", align_bytes=ALIGN)
         nc.vector.quantize_mx(out=w1_codes[:].bitcast(FP8X4), scales=w1_plane[:], in_=w1_bf[:])

@@ -25,6 +25,7 @@ SUB = 128
 SCALE_ROW0 = 112
 H_BANKS = 4
 ALIGN = 256
+HALF = S // 2
 
 
 def tile_list_tabres_bias_kernel(
@@ -36,8 +37,7 @@ def tile_list_tabres_bias_kernel(
         shared = ctx.enter_context(tc.tile_pool(name="shared", bufs=1))
         psum = ctx.enter_context(tc.psum_pool(name="psum", bufs=1))
 
-        res_bytes = T * 4
-        scale_win = shared.tile([P, T // 4], I32, name="scale_win", offset=res_bytes - ALIGN, align_bytes=ALIGN)
+        scale_win = keep.tile([P, T // 4], I32, name="scale_win", align_bytes=ALIGN)
         nc.sync.dma_start(scale_win[SCALE_ROW0:P, :], tab_scales[0].bitcast(I32))
         offsets = keep.tile([P, S // LANES], U16, name="offsets")
         nc.sync.dma_start(offsets[:], offs)
@@ -48,14 +48,15 @@ def tile_list_tabres_bias_kernel(
         w2_plane = keep.tile([P, M // 4], I32, name="w2_plane", align_bytes=ALIGN)
         nc.vector.memset(w2_plane[:], 0)
         nc.vector.memset(scale_win[0:SCALE_ROW0, :], 0)
-        tok_plane = keep.tile([P, S // 4], I32, name="tok_plane", align_bytes=ALIGN)
-        nc.vector.memset(tok_plane[:], 0)
+        tok_planes = {}
+        for lo in (0, HALF):
+            tok_planes[lo] = keep.tile([P, HALF // 4], I32, name=f"tok_plane{lo}", align_bytes=ALIGN)
+            nc.vector.memset(tok_planes[lo][:], 0)
 
         w1_raw = keep.tile([P, PACK, H], F32, name="w1_raw", align_bytes=ALIGN)
         nc.sync.dma_start(w1_raw[:], w1.rearrange("(p j) r -> p j r", j=PACK))
-        w2_scale_rows = w2_scales[0].bitcast(I32)
-        for r in range(4):
-            nc.sync.dma_start(w2_plane[r:P:32, :], w2_scale_rows[r:16:4, :])
+        w2_staged = keep.tile([4, 4, M // 4], I32, name="w2_staged", align_bytes=ALIGN)
+        nc.sync.dma_start(w2_staged[:], w2_scales[0].bitcast(I32).rearrange("(q i) c -> i q c", q=4))
         word_win = keep.tile([P, T], I32, name="word_win", align_bytes=ALIGN)
         nc.sync.dma_start(word_win[:], tab_words[0].rearrange("p t i -> p (t i)").bitcast(I32))
         w2_codes = keep.tile([P, 2 * M // 4], I32, name="w2_codes", align_bytes=ALIGN)
@@ -63,20 +64,26 @@ def tile_list_tabres_bias_kernel(
         bias = keep.tile([P, 1], F32, name="bias", align_bytes=ALIGN)
         nc.sync.dma_start(bias[:], b.rearrange("(p o) -> p o", o=1))
 
-        picked_scales = keep.tile([P, S], U8, name="picked_scales", align_bytes=ALIGN)
-        nc.vector.tensor_copy(picked_scales[:], scale_win[:].bitcast(U8).indirect(picks(0, S)))
-        for r in range(4):
-            nc.sync.dma_start(tok_plane[r:P:32, :], picked_scales[:].bitcast(I32)[SCALE_ROW0 + r : P : 4, :])
-        tok_scales = tok_plane[:].bitcast(U8)
+        picked = {}
+        for lo in (0, HALF):
+            picked[lo] = keep.tile([P, HALF], U8, name=f"picked{lo}", align_bytes=ALIGN)
+            nc.vector.tensor_copy(picked[lo][:], scale_win[:].bitcast(U8).indirect(picks(lo, lo + HALF)))
 
-        res_win = shared.tile([P, T], F32, name="res_win", offset=0, align_bytes=ALIGN)
+        def move_scales(lo):
+            for r in range(4):
+                nc.sync.dma_start(tok_planes[lo][r:P:32, :], picked[lo][:].bitcast(I32)[SCALE_ROW0 + r : P : 4, :])
+
+        move_scales(0)
+        res_win = keep.tile([P, T], F32, name="res_win", align_bytes=ALIGN)
         nc.sync.dma_start(res_win[:], rT)
+        move_scales(HALF)
 
         w1_bf = keep.tile([P, H * PACK], BF16, name="w1_bf", align_bytes=ALIGN)
         cast_to = w1_bf[:].rearrange("p (t m j) -> p m t j", t=PACK, j=PACK)
         cast_from = w1_raw[:].rearrange("p j (m t) -> p m t j", t=PACK)
-        nc.scalar.copy(cast_to[:, :96], cast_from[:, :96])
-        nc.vector.tensor_copy(cast_to[:, 96:], cast_from[:, 96:])
+        nc.scalar.copy(cast_to, cast_from)
+        for q in range(4):
+            nc.vector.tensor_copy(w2_plane[32 * q : 32 * q + 4, :], w2_staged[:, q, :])
         w1_codes = keep.tile([P, H], U32, name="w1_codes", align_bytes=ALIGN)
         w1_plane = keep.tile([P, H], U8, name="w1_plane", align_bytes=ALIGN)
         nc.vector.quantize_mx(out=w1_codes[:].bitcast(FP8X4), scales=w1_plane[:], in_=w1_bf[:])
@@ -89,7 +96,7 @@ def tile_list_tabres_bias_kernel(
         y_banks = {}
         res = {}
         y_out = keep.tile([P, S], F32, name="y_out", align_bytes=ALIGN)
-        total = keep.tile([P, S], F32, name="total", align_bytes=ALIGN)
+        total = {}
 
         def new_tile(name, width, dtype, place):
             if isinstance(place, int):
@@ -114,7 +121,7 @@ def tile_list_tabres_bias_kernel(
                         lhsT=w1_codes[:, ch].bitcast(FP8X4),
                         lhsT_scale=w1_plane[:, ch],
                         rhs=part(words, s0, s0 + SUB).bitcast(FP8X4),
-                        rhs_scale=tok_scales[:, s0 : s0 + SUB],
+                        rhs_scale=tok_planes[s0 // HALF * HALF][:].bitcast(U8)[:, s0 % HALF : s0 % HALF + SUB],
                         start=True,
                         stop=True,
                     )
@@ -166,39 +173,36 @@ def tile_list_tabres_bias_kernel(
         def store(lo, hi, pieces):
             width = (hi - lo) // pieces
             for s0 in range(lo, hi, width):
-                nc.sync.dma_start(out[:, s0 : s0 + width], total[:, s0 : s0 + width])
+                nc.sync.dma_start(out[:, s0 : s0 + width], part(total, s0, s0 + width))
 
-        def sum_in_gather(lo, hi, pieces=1):
-            nc.vector.tensor_tensor(total[:, lo:hi], res_win[:].indirect(picks(lo, hi)), y_out[:, lo:hi], ADD)
+        def sum_in_gather(lo, hi, pieces=1, place=None):
+            total[lo] = new_tile(f"total{lo}", hi - lo, F32, place or f"total{lo}")
+            nc.vector.tensor_tensor(total[lo][:], res_win[:].indirect(picks(lo, hi)), y_out[:, lo:hi], ADD)
             store(lo, hi, pieces)
 
-        def sum_on_gpsimd(lo, hi, pieces=1):
-            nc.gpsimd.tensor_tensor(total[:, lo:hi], y_out[:, lo:hi], part(res, lo, hi), ADD)
-            store(lo, hi, pieces)
-
-        def sum_from_bank(lo, hi, pieces=1):
-            nc.vector.scalar_tensor_tensor(total[:, lo:hi], part(y_banks, lo, hi), bias[:], part(res, lo, hi), ADD, ADD)
+        def sum_from_bank(lo, hi, pieces=1, place=None):
+            total[lo] = new_tile(f"total{lo}", hi - lo, F32, place or f"total{lo}")
+            nc.vector.scalar_tensor_tensor(total[lo][:], part(y_banks, lo, hi), bias[:], part(res, lo, hi), ADD, ADD)
             store(lo, hi, pieces)
 
         gather_words(0, 256, "words0")
         gather_words(256, 768, "words1")
-        gather_words(768, 1536, "words2")
+        gather_words(768, 1536, 0)
         gather_words(1536, 2048, "words3")
         make_h(0, 512)
         quantise_h(0, 512, "plane0")
         make_y(0, 512, 4)
         make_h(512, 768)
-        quantise_h(512, 768, "plane1")
         gather_residual(896, 1792, "res")
         make_h(768, 1024)
         bring_out(0, 512)
         make_h(1024, 1536)
-        quantise_h(768, 1024, "words2")
+        quantise_h(512, 1024, 0)
         open_bank(512, 896, 5)
         second_product(512, 768)
         second_product(768, 896)
         make_y(896, 1024, 6)
-        sum_in_gather(0, 512, 2)
+        sum_in_gather(0, 512, 1, 2 * ALIGN)
         sum_from_bank(896, 1024)
         bring_out(512, 896)
         quantise_h(1024, 1536, "plane2")

@@ -25,7 +25,7 @@ SUB = 128
 SCALE_ROW0 = 112
 H_BANKS = 4
 ALIGN = 256
-HALF = S // 2
+SCALE_CUTS = ((0, 1536), (1536, S))
 
 
 def tile_list_tabres_bias_kernel(
@@ -49,8 +49,8 @@ def tile_list_tabres_bias_kernel(
         nc.vector.memset(w2_plane[:], 0)
         nc.vector.memset(scale_win[0:SCALE_ROW0, :], 0)
         tok_planes = {}
-        for lo in (0, HALF):
-            tok_planes[lo] = keep.tile([P, HALF // 4], I32, name=f"tok_plane{lo}", align_bytes=ALIGN)
+        for lo, hi in SCALE_CUTS:
+            tok_planes[lo] = keep.tile([P, (hi - lo) // 4], I32, name=f"tok_plane{lo}", align_bytes=ALIGN)
             nc.vector.memset(tok_planes[lo][:], 0)
 
         w1_raw = keep.tile([P, PACK, H], F32, name="w1_raw", align_bytes=ALIGN)
@@ -65,9 +65,9 @@ def tile_list_tabres_bias_kernel(
         nc.sync.dma_start(bias[:], b.rearrange("(p o) -> p o", o=1))
 
         picked = {}
-        for lo in (0, HALF):
-            picked[lo] = keep.tile([P, HALF], U8, name=f"picked{lo}", align_bytes=ALIGN)
-            nc.vector.tensor_copy(picked[lo][:], scale_win[:].bitcast(U8).indirect(picks(lo, lo + HALF)))
+        for lo, hi in SCALE_CUTS:
+            picked[lo] = keep.tile([P, hi - lo], U8, name=f"picked{lo}", align_bytes=ALIGN)
+            nc.vector.tensor_copy(picked[lo][:], scale_win[:].bitcast(U8).indirect(picks(lo, hi)))
 
         def move_scales(lo):
             for r in range(4):
@@ -76,7 +76,8 @@ def tile_list_tabres_bias_kernel(
         move_scales(0)
         res_win = keep.tile([P, T], F32, name="res_win", align_bytes=ALIGN)
         nc.sync.dma_start(res_win[:], rT)
-        move_scales(HALF)
+        move_scales(SCALE_CUTS[1][0])
+        tok_scales = {lo: plane[:].bitcast(U8) for lo, plane in tok_planes.items()}
 
         w1_bf = keep.tile([P, H * PACK], BF16, name="w1_bf", align_bytes=ALIGN)
         cast_to = w1_bf[:].rearrange("p (t m j) -> p m t j", t=PACK, j=PACK)
@@ -121,7 +122,7 @@ def tile_list_tabres_bias_kernel(
                         lhsT=w1_codes[:, ch].bitcast(FP8X4),
                         lhsT_scale=w1_plane[:, ch],
                         rhs=part(words, s0, s0 + SUB).bitcast(FP8X4),
-                        rhs_scale=tok_planes[s0 // HALF * HALF][:].bitcast(U8)[:, s0 % HALF : s0 % HALF + SUB],
+                        rhs_scale=part(tok_scales, s0, s0 + SUB),
                         start=True,
                         stop=True,
                     )

from contextlib import ExitStack

import concourse.mybir as mybir

K, H, M, T, S = 512, 512, 128, 4096, 2048
FLOPS = 2 * K * H * S + 2 * H * M * S

F32 = mybir.dt.float32
BF16 = mybir.dt.bfloat16
I32 = mybir.dt.int32
U32 = mybir.dt.uint32
U16 = mybir.dt.uint16
U8 = mybir.dt.uint8
FP8X4 = mybir.dt.float8_e4m3fn_x4
FP4X4 = mybir.dt.float4_e2m1fn_x4
ADD = mybir.AluOpType.add
IDENTITY = mybir.ActivationFunctionType.Identity
RELU = mybir.ActivationFunctionType.Relu

P = 128
PACK = 4
LANES = 16
CHUNK = 512
SUB = 128
SCALE_ROW0 = 112
H_BANKS = 4
ALIGN = 256
SCALE_CUTS = ((0, 1536), (1536, S))


def tile_list_tabres_bias_kernel(
    tc, tab_words, tab_scales, w1, w2_words, w2_scales, rT, b, offs, out
):
    nc = tc.nc
    with ExitStack() as ctx:
        keep = ctx.enter_context(tc.tile_pool(name="keep", bufs=1))
        shared = ctx.enter_context(tc.tile_pool(name="shared", bufs=1))
        psum = ctx.enter_context(tc.psum_pool(name="psum", bufs=1))

        scale_win = keep.tile([P, T // 4], I32, name="scale_win", align_bytes=ALIGN)
        nc.sync.dma_start(scale_win[SCALE_ROW0:P, :], tab_scales[0].bitcast(I32))
        offsets = keep.tile([P, S // LANES], U16, name="offsets")
        nc.sync.dma_start(offsets[:], offs)

        def picks(lo, hi):
            return offsets[:, lo // LANES : hi // LANES]

        w2_plane = keep.tile([P, M // 4], I32, name="w2_plane", align_bytes=ALIGN)
        nc.vector.memset(w2_plane[:], 0)
        nc.vector.memset(scale_win[0:SCALE_ROW0, :], 0)
        tok_planes = {}
        for lo, hi in SCALE_CUTS:
            tok_planes[lo] = keep.tile([P, (hi - lo) // 4], I32, name=f"tok_plane{lo}", align_bytes=ALIGN)
            nc.vector.memset(tok_planes[lo][:], 0)

        w1_raw = keep.tile([P, PACK, H], F32, name="w1_raw", align_bytes=ALIGN)
        nc.sync.dma_start(w1_raw[:], w1.rearrange("(p j) r -> p j r", j=PACK))
        w2_staged = keep.tile([4, 4, M // 4], I32, name="w2_staged", align_bytes=ALIGN)
        nc.sync.dma_start(w2_staged[:], w2_scales[0].bitcast(I32).rearrange("(q i) c -> i q c", q=4))
        word_win = keep.tile([P, T], I32, name="word_win", align_bytes=ALIGN)
        nc.sync.dma_start(word_win[:], tab_words[0].rearrange("p t i -> p (t i)").bitcast(I32))
        w2_codes = keep.tile([P, 2 * M // 4], I32, name="w2_codes", align_bytes=ALIGN)
        nc.sync.dma_start(w2_codes[:], w2_words[0].bitcast(I32))
        bias = keep.tile([P, 1], F32, name="bias", align_bytes=ALIGN)
        nc.sync.dma_start(bias[:], b.rearrange("(p o) -> p o", o=1))

        picked = {}
        for lo, hi in SCALE_CUTS:
            picked[lo] = keep.tile([P, hi - lo], U8, name=f"picked{lo}", align_bytes=ALIGN)
            nc.vector.tensor_copy(picked[lo][:], scale_win[:].bitcast(U8).indirect(picks(lo, hi)))

        def move_scales(lo):
            for r in range(4):
                nc.sync.dma_start(tok_planes[lo][r:P:32, :], picked[lo][:].bitcast(I32)[SCALE_ROW0 + r : P : 4, :])

        move_scales(0)
        res_win = keep.tile([P, T], F32, name="res_win", align_bytes=ALIGN)
        nc.sync.dma_start(res_win[:], rT)
        move_scales(SCALE_CUTS[1][0])
        tok_scales = {lo: plane[:].bitcast(U8) for lo, plane in tok_planes.items()}

        w1_bf = keep.tile([P, H * PACK], BF16, name="w1_bf", align_bytes=ALIGN)
        cast_to = w1_bf[:].rearrange("p (t m j) -> p m t j", t=PACK, j=PACK)
        cast_from = w1_raw[:].rearrange("p j (m t) -> p m t j", t=PACK)
        nc.scalar.copy(cast_to, cast_from)
        for q in range(4):
            nc.vector.tensor_copy(w2_plane[32 * q : 32 * q + 4, :], w2_staged[:, q, :])
        w1_codes = keep.tile([P, H], U32, name="w1_codes", align_bytes=ALIGN)
        w1_plane = keep.tile([P, H], U8, name="w1_plane", align_bytes=ALIGN)
        nc.vector.quantize_mx(out=w1_codes[:].bitcast(FP8X4), scales=w1_plane[:], in_=w1_bf[:])

        words = {}
        h_banks = {}
        h_bf = {c: keep.tile([P, CHUNK * PACK], BF16, name=f"h_bf{c}", align_bytes=ALIGN) for c in range(0, S, CHUNK)}
        h_codes = keep.tile([P, S], U32, name="h_codes", align_bytes=ALIGN)
        planes = {}
        y_banks = {}
        res = {}
        y_out = keep.tile([P, S], F32, name="y_out", align_bytes=ALIGN)
        total = {}

        def new_tile(name, width, dtype, place):
            if isinstance(place, int):
                return shared.tile([P, width], dtype, name=name, offset=place, align_bytes=ALIGN)
            return keep.tile([P, width], dtype, name=name, tag=place, align_bytes=ALIGN)

        def part(tiles, lo, hi, width=1):
            base = max(k for k in tiles if k <= lo)
            return tiles[base][:, (lo - base) * width : (hi - base) * width]

        def gather_words(lo, hi, tag):
            words[lo] = new_tile(f"words{lo}", hi - lo, U32, tag)
            nc.vector.tensor_copy(words[lo][:], word_win[:].bitcast(U32).indirect(picks(lo, hi)))

        def first_product(lo, hi, bank=None):
            for s0 in range(lo, hi, SUB):
                h_banks[s0] = psum.tile([P, PACK, SUB], F32, name="h_bank", tag=f"bank{len(h_banks) % H_BANKS if bank is None else bank}")
                for t in range(PACK):
                    ch = slice(t * P, (t + 1) * P)
                    nc.tensor.matmul_mx(
                        out=h_banks[s0][:, t, :],
                        lhsT=w1_codes[:, ch].bitcast(FP8X4),
                        lhsT_scale=w1_plane[:, ch],
                        rhs=part(words, s0, s0 + SUB).bitcast(FP8X4),
                        rhs_scale=part(tok_scales, s0, s0 + SUB),
                        start=True,
                        stop=True,
                    )

        def relu(lo, hi):
            for s0 in range(lo, hi, SUB):
                nc.scalar.activation(
                    part(h_bf, s0, s0 + SUB, PACK).rearrange("p (n t) -> p n t", t=PACK),
                    h_banks[s0][:].rearrange("p t n -> p n t"),
                    RELU,
                )

        def make_h(lo, hi, bank=None):
            for s0 in range(lo, hi, SUB):
                first_product(s0, s0 + SUB, bank)
                relu(s0, s0 + SUB)

        def quantise_h(lo, hi, plane_tag):
            planes[lo] = new_tile(f"plane{lo}", hi - lo, U8, plane_tag)
            nc.vector.quantize_mx(
                out=h_codes[:, lo:hi].bitcast(FP8X4), scales=planes[lo][:], in_=part(h_bf, lo, hi, PACK)
            )

        def open_bank(lo, hi, bank):
            y_banks[lo] = psum.tile([P, hi - lo], F32, name=f"y_bank{lo}", tag=f"bank{bank}")

        def second_product(lo, hi):
            nc.tensor.matmul_mx(
                out=part(y_banks, lo, hi),
                lhsT=w2_codes[:].bitcast(U8).bitcast(FP4X4),
                lhsT_scale=w2_plane[:].bitcast(U8),
                rhs=h_codes[:, lo:hi].bitcast(FP8X4),
                rhs_scale=part(planes, lo, hi),
                start=True,
                stop=True,
            )

        def make_y(lo, hi, bank):
            open_bank(lo, hi, bank)
            second_product(lo, hi)

        def gather_residual(lo, hi, place):
            res[lo] = new_tile(f"res{lo}", hi - lo, F32, place)
            nc.vector.tensor_copy(res[lo][:], res_win[:].indirect(picks(lo, hi)))

        def bring_out(lo, hi):
            nc.scalar.activation(y_out[:, lo:hi], part(y_banks, lo, hi), IDENTITY, bias=bias[:])

        def store(lo, hi, pieces):
            width = (hi - lo) // pieces
            for s0 in range(lo, hi, width):
                nc.sync.dma_start(out[:, s0 : s0 + width], part(total, s0, s0 + width))

        def sum_in_gather(lo, hi, pieces=1, place=None):
            total[lo] = new_tile(f"total{lo}", hi - lo, F32, place or f"total{lo}")
            nc.vector.tensor_tensor(total[lo][:], res_win[:].indirect(picks(lo, hi)), y_out[:, lo:hi], ADD)
            store(lo, hi, pieces)

        def sum_from_bank(lo, hi, pieces=1, place=None):
            total[lo] = new_tile(f"total{lo}", hi - lo, F32, place or f"total{lo}")
            nc.vector.scalar_tensor_tensor(total[lo][:], part(y_banks, lo, hi), bias[:], part(res, lo, hi), ADD, ADD)
            store(lo, hi, pieces)

        gather_words(0, 256, "words0")
        gather_words(256, 768, "words1")
        gather_words(768, 1536, 0)
        gather_words(1536, 2048, "words3")
        make_h(0, 512)
        quantise_h(0, 512, "plane0")
        make_y(0, 512, 4)
        make_h(512, 768)
        gather_residual(896, 1792, "res")
        make_h(768, 1024)
        bring_out(0, 512)
        make_h(1024, 1536)
        quantise_h(512, 1024, 0)
        open_bank(512, 896, 5)
        second_product(512, 768)
        second_product(768, 896)
        make_y(896, 1024, 6)
        sum_in_gather(0, 512, 1, 2 * ALIGN)
        sum_from_bank(896, 1024)
        bring_out(512, 896)
        quantise_h(1024, 1536, "plane2")
        sum_in_gather(512, 896)
        make_h(1792, 2048)
        quantise_h(1792, 2048, "plane3")
        make_y(1024, 1280, 1)
        make_y(1792, 2048, 6)
        sum_from_bank(1024, 1280)
        make_h(1536, 1664, 3)
        quantise_h(1536, 1664, "plane4")
        make_y(1280, 1536, 3)
        make_y(1536, 1664, 5)
        sum_from_bank(1280, 1536)
        make_h(1664, 1792, 0)
        quantise_h(1664, 1792, "plane5")
        make_y(1664, 1792, 7)
        bring_out(1792, 2048)
        sum_from_bank(1536, 1664)
        sum_in_gather(1792, 2048)
        sum_from_bank(1664, 1792)
